import numpy as np
import ml_dtypes


def mxq(x, axis, fmt="e4m3"):
    dtype, down = {"e4m3": (ml_dtypes.float8_e4m3fn, 7), "e5m2": (ml_dtypes.float8_e5m2, 14)}[fmt]
    v = np.moveaxis(np.asarray(x, np.float32).astype(ml_dtypes.bfloat16).astype(np.float64), axis, -1)
    blocks = v.reshape(v.shape[:-1] + (-1, 32))
    amax = np.abs(blocks).max(-1, keepdims=True)
    byte = np.maximum(np.where(amax > 0, np.frexp(amax)[1] - 1 + 127, 0) - down, 1)
    scale = np.exp2(byte - 127.0)
    codes = (blocks / scale).astype(np.float32).astype(dtype).astype(np.float64)
    return np.moveaxis((codes * scale).reshape(v.shape), -1, axis)


WIDE = False


def mx_kscale(k):
    if not WIDE:
        return np.ones(k)
    levels = np.array([10, -10, 5, -5, 0])
    if k % 512:
        return np.exp2(np.random.permutation(np.resize(levels, k // 32))).repeat(32)
    a = np.empty((k // 512, 16))
    for p in range(k // 512):
        a[p, :8] = np.random.permutation(np.resize(levels, 8))
        for g in range(8):
            far = levels[np.abs(levels - a[p, g]) >= 10]
            a[p, g + 8] = far[np.random.randint(len(far))]
    return np.exp2(a.ravel()).repeat(32)


BF16 = ml_dtypes.bfloat16


def bf(x):
    return np.asarray(x, np.float32).astype(BF16)


def f64(x):
    return np.asarray(x).astype(np.float64)

def planes(Y):
    n, m = Y.shape
    b = f64(bf(Y)).reshape(n // 32, 32, m)
    amax = np.abs(b).max(1)
    byte = np.clip(np.where(amax > 0, np.frexp(amax)[1] - 1 + 127 - 7, 1), 1, 254)
    codes = (b * np.exp2(127.0 - byte)[:, None, :]).reshape(n, m).astype(np.float32).astype(ml_dtypes.float8_e4m3fn).view(np.uint8)
    words = codes.reshape(n // 512, 128, 4, m).transpose(0, 1, 3, 2)
    return np.ascontiguousarray(words), np.ascontiguousarray(byte.astype(np.uint8).reshape(n // 512, 16, m))


B, D, R, E = 1024, 1024, 512, 2


def softmax(g):
    e = np.exp(g - g.max(axis=-1, keepdims=True))
    return e / e.sum(axis=-1, keepdims=True)


def setup_inputs():
    s, t = mx_kscale(D), mx_kscale(R)
    x0 = bf(np.random.standard_normal((B, D)) * s)
    x = bf(np.random.standard_normal((B, D)) * s)
    v = bf(np.random.standard_normal((E, D, R)) / np.sqrt(D) / s[None, :, None])
    c = bf((1.0 + 0.1 * np.random.standard_normal((E, R))) * t)
    u = bf(1.5 * np.random.standard_normal((E, R, D)) / np.sqrt(R) / t[None, :, None])
    bias = bf(0.3 * np.random.standard_normal(D))
    gate_logits = bf(np.random.standard_normal((B, E)))
    return {"x0": x0, "x": x, "v": v, "c": c, "u": u, "bias": bias, "gate_logits": gate_logits}


def expert_outputs(x, v, c, u):
    a = mxq(x, 1, "e4m3") @ mxq(v, 1, "e4m3")
    h = np.tanh(a) * c[:, None, :]
    return mxq(h, 2, "e4m3") @ mxq(u, 1, "e4m3")


def core(x0, x, v, c, u, bias, gate_logits):
    y = expert_outputs(f64(x), f64(v), f64(c), f64(u))
    p = softmax(f64(gate_logits))
    weights = np.transpose(p)[:, :, None]
    m = np.sum(weights * y, axis=0)
    return f64(x0) * (m + f64(bias)[None, :]) + f64(x)


def reference(x0, x, v, c, u, bias, gate_logits):
    R_out = core(x0, x, v, c, u, bias, gate_logits)
    words, scales = planes(R_out.T)
    return R_out, words, scales

@@ -1,0 +1,442 @@
+from contextlib import ExitStack
+
+import concourse.mybir as mybir
+from concourse.masks import make_identity
+
+B, D, R, E = 1024, 1024, 512, 2
+FLOPS = 2 * 2 * E * B * D * R
+
+F32 = mybir.dt.float32
+BF16 = mybir.dt.bfloat16
+U32 = mybir.dt.uint32
+I32 = mybir.dt.int32
+U8 = mybir.dt.uint8
+FP8X4 = mybir.dt.float8_e4m3fn_x4
+ALU = mybir.AluOpType
+ACT = mybir.ActivationFunctionType
+P = 128
+
+GS = 768
+FORM3 = {(0, 2), (1, 2), (0, 3), (1, 3)}
+SSET = {}
+V_ROUTE = {(0, 0): "V", (0, 1): "V", (1, 0): "V", (1, 1): "PE"}
+U_ROUTE = {(0, 0): "PE", (1, 0): "PE", (0, 1): "S", (1, 1): "S"}
+
+
+def tile_dcnv2lowrankexpertcross_x1_kernel(tc, x0, x, v, c, u, bias, gate, out, words, scales):
+    nc = tc.nc
+    with ExitStack() as ctx:
+        keep = ctx.enter_context(tc.tile_pool(name="keep", bufs=1))
+        work = ctx.enter_context(tc.tile_pool(name="work", bufs=2))
+        psum = ctx.enter_context(tc.psum_pool(name="psum", bufs=1))
+
+        xs = keep.tile([P, 8, D], BF16, name="xs", align_bytes=64)
+        x0s = keep.tile([P, 8, D], BF16, name="x0s", align_bytes=64)
+        vraw, vg, vc, vs = {}, {}, {}, {}
+        uraw, ug, uc, us = {}, {}, {}, {}
+        for e in range(E):
+            for g in range(2):
+                vraw[e, g] = keep.tile([P, 4, R], BF16, name=f"vraw{e}{g}", align_bytes=64)
+                vg[e, g] = keep.tile([P, 4 * R], BF16, name=f"vg{e}{g}", align_bytes=64)
+                vc[e, g] = keep.tile([P, R], U32, name=f"vc{e}{g}", align_bytes=64)
+                vs[e, g] = keep.tile([P, R], U8, name=f"vs{e}{g}", align_bytes=64)
+                uraw[e, g] = keep.tile([P, 4, 512], BF16, name=f"uraw{e}{g}", align_bytes=64)
+                ug[e, g] = keep.tile([P, 512, 4], BF16, name=f"ug{e}{g}", align_bytes=64)
+                uc[e, g] = keep.tile([P, 512], U32, name=f"uc{e}{g}", align_bytes=64)
+                us[e, g] = keep.tile([P, 512], U8, name=f"us{e}{g}", align_bytes=64)
+        xg = [keep.tile([P, 2, 256, 2], F32, name=f"xg{h}", align_bytes=64) for h in range(4)]
+        xc = [keep.tile([P, 2, 256], U32, name=f"xc{h}", align_bytes=64) for h in range(4)]
+        xsc = [keep.tile([P, 2, 256], U8, name=f"xsc{h}", align_bytes=64) for h in range(4)]
+        hc = {(e, h): keep.tile([P, 256], U32, name=f"hc{e}{h}", align_bytes=64) for e in range(E) for h in range(4)}
+        hs = {(e, h): keep.tile([P, 256], U8, name=f"hs{e}{h}", align_bytes=64) for e in range(E) for h in range(4)}
+        osc = [keep.tile([P, 2, 512], U8, name=f"osc{h}", align_bytes=64) for h in range(2)]
+        cf = keep.tile([P, E, 4], F32, name="cf")
+        csb = keep.tile([P, E, 4], BF16, name="csb")
+        graw = keep.tile([P, 8, E], BF16, name="graw")
+        gmx = keep.tile([P, 8], F32, name="gmx")
+        gd = keep.tile([P, 8, E], F32, name="gd")
+        ge = keep.tile([P, 8, E], F32, name="ge")
+        gsum = keep.tile([P, 8], F32, name="gsum")
+        grec = keep.tile([P, 8], F32, name="grec")
+        gp = keep.tile([P, 8, E], F32, name="gp")
+        bpad = keep.tile([P, D], BF16, name="bpad")
+        ones = keep.tile([P, P], BF16, name="ones")
+        biasb = keep.tile([P, D], F32, name="biasb")
+        idf = keep.tile([P, P], F32, name="idf")
+        idb = keep.tile([P, P], BF16, name="idb")
+        warm = keep.tile([P, 8], F32, name="warm")
+
+        def bank(tag, bufs, dtype=F32, name=None):
+            return psum.tile([P, 512 if dtype == F32 else 1024], dtype, name=name or tag, tag=tag, bufs=bufs)
+
+        def load_x(dst, src, i):
+            nc.sync.dma_start(out=dst[:, i, :], in_=src[i * P : (i + 1) * P, :])
+
+        def load_v(e, g):
+            nc.sync.dma_start(out=vraw[e, g][:], in_=v[e, g * 512 : (g + 1) * 512, :].rearrange("(p j) w -> p j w", j=4))
+
+        def load_u(e, dh):
+            nc.sync.dma_start(
+                out=uraw[e, dh][:],
+                in_=u[e, :, dh * 512 : (dh + 1) * 512].rearrange("(p j) w -> p j w", j=4),
+            )
+
+        nc.gpsimd.memset(warm[:], 0.0)
+        make_identity(nc, idf[:])
+        make_identity(nc, idb[:])
+        nc.gpsimd.memset(ones[:], 1.0)
+        nc.gpsimd.memset(bpad[:], 0.0)
+        nc.scalar.activation(out=warm[:], in_=warm[:], func=ACT.Tanh)
+
+        for q in range(2):
+            cols = slice(256 * q, 256 * (q + 1))
+            nc.sync.dma_start(
+                out=vraw[0, 0][:, :, cols], in_=v[0, :512, cols].rearrange("(p j) w -> p j w", j=4)
+            )
+        load_x(xs, x, 0)
+        load_x(xs, x, 1)
+        load_v(0, 1)
+        nc.sync.dma_start(out=csb[:], in_=c.rearrange("e (p t) -> p e t", t=4))
+        nc.sync.dma_start(out=bpad[0:1, :], in_=bias.unsqueeze(0))
+        load_v(1, 0)
+        load_v(1, 1)
+        load_u(0, 0)
+        nc.sync.dma_start(out=graw[:], in_=gate.rearrange("(i p) e -> p i e", p=P))
+        load_u(1, 0)
+        load_x(xs, x, 2)
+        load_x(xs, x, 3)
+        load_x(x0s, x0, 0)
+        load_x(x0s, x0, 1)
+        load_u(0, 1)
+        load_u(1, 1)
+        for i in (2, 3):
+            load_x(x0s, x0, i)
+        for i in range(4, 8):
+            load_x(xs, x, i)
+        for i in range(4, 8):
+            load_x(x0s, x0, i)
+
+        def x_turn(i):
+            tr = bank("tr", 2)
+            trv = tr[:].rearrange("p (g u r) -> p g u r", g=2, u=2)
+            xw = xs[:, i, :].bitcast(F32)
+            for g in range(2):
+                for w in range(2):
+                    nc.tensor.transpose(trv[:, g, w, :], xw[:, 256 * g + w : 256 * (g + 1) : 2], idf[:])
+            li = i % 2
+            nc.scalar.copy(
+                out=xg[i // 2][:, :, li * P : (li + 1) * P, :], in_=tr[:].rearrange("p (g u r) -> p g r u", g=2, u=2)
+            )
+
+        def x_quant(h):
+            nc.vector.quantize_mx(
+                out=xc[h][:].rearrange("p g b -> p (g b)").bitcast(FP8X4),
+                scales=xsc[h][:].rearrange("p g b -> p (g b)"),
+                in_=xg[h][:].rearrange("p g b u -> p (g b u)").bitcast(BF16),
+            )
+
+        TB = {"y": 4, "aux": 2, "tr": 2}
+
+        def interleave(route, raw, dst_half, pat, tag):
+            for q in range(2):
+                cols = slice(256 * q, 256 * (q + 1))
+                if route == "PE":
+                    mv = bank(tag, TB[tag], BF16, name="mv")
+                    mvv = mv[:].rearrange("p (j c) -> p j c", j=4)
+                    for k in range(2):
+                        nc.tensor.matmul(
+                            mvv[:, 2 * k : 2 * k + 2, :], lhsT=idb[:], rhs=raw[:, 2 * k : 2 * k + 2, cols], start=True, stop=True
+                        )
+                    nc.scalar.copy(out=dst_half(q), in_=mvv.rearrange(pat[0], **pat[1]))
+                elif route == "S":
+                    nc.scalar.copy(out=dst_half(q), in_=raw[:, :, cols].rearrange(pat[0], **pat[1]))
+                else:
+                    nc.vector.tensor_copy(out=dst_half(q), in_=raw[:, :, cols].rearrange(pat[0], **pat[1]))
+
+        def v_inter(e, g):
+            dst = vg[e, g][:].rearrange("p (t m j) -> p t m j", t=4, j=4)
+            interleave(
+                V_ROUTE[e, g], vraw[e, g], lambda q: dst[:, :, 64 * q : 64 * (q + 1), :], ("p j (m t) -> p t m j", {"t": 4}), "y"
+            )
+
+        def v_quant(e, g):
+            nc.vector.quantize_mx(out=vc[e, g][:].bitcast(FP8X4), scales=vs[e, g][:], in_=vg[e, g][:])
+
+        def u_inter(e, dh):
+            interleave(
+                U_ROUTE[e, dh], uraw[e, dh], lambda q: ug[e, dh][:, 256 * q : 256 * (q + 1), :], ("p j c -> p c j", {}), "y" if dh == 0 else "aux"
+            )
+
+        def u_quant(e, dh):
+            nc.vector.quantize_mx(
+                out=uc[e, dh][:].bitcast(FP8X4), scales=us[e, dh][:], in_=ug[e, dh][:].rearrange("p c j -> p (c j)")
+            )
+
+        th = {}
+
+        def stage1(e, h):
+            th[e, h] = work.tile([P, 4, 256], F32, name="th", tag="th", bufs=4)
+            for q in range(2):
+                acc = bank("aux", 2, name="a1")
+                for k in range(2):
+                    t = 2 * q + k
+                    for g in range(2):
+                        nc.tensor.matmul_mx(
+                            out=acc[:, 256 * k : 256 * (k + 1)],
+                            lhsT=vc[e, g][:, t * P : (t + 1) * P].bitcast(FP8X4),
+                            lhsT_scale=vs[e, g][:, t * P : (t + 1) * P],
+                            rhs=xc[h][:, g, :].bitcast(FP8X4),
+                            rhs_scale=xsc[h][:, g, :],
+                            start=(g == 0),
+                            stop=(g == 1),
+                        )
+                nc.scalar.activation(
+                    out=th[e, h][:, 2 * q : 2 * q + 2, :].rearrange("p t b -> p (t b)"), in_=acc[:], func=ACT.Tanh
+                )
+
+        hb = {}
+
+        def h_mult(e, h):
+            hb[e, h] = work.tile([P, 256, 4], BF16, name="hb", tag="hb", bufs=3, align_bytes=64)
+            if (e, h) in FORM3 or (e, h) in SSET:
+                ht = work.tile([P, 4, 256], BF16, name="ht", tag="ht")
+                for t in range(4):
+                    nc.scalar.activation(out=ht[:, t, :], in_=th[e, h][:, t, :], func=ACT.Copy, scale=cf[:, e, t : t + 1])
+                if (e, h) in SSET:
+                    nc.scalar.copy(out=hb[e, h][:], in_=ht[:].rearrange("p t b -> p b t"))
+                else:
+                    mv = bank("aux", 2, BF16, name="mv")
+                    mvv = mv[:].rearrange("p (t b) -> p t b", t=4)
+                    for k in range(2):
+                        nc.tensor.matmul(
+                            mvv[:, 2 * k : 2 * k + 2, :], lhsT=idb[:], rhs=ht[:, 2 * k : 2 * k + 2, :], start=True, stop=True
+                        )
+                    nc.scalar.copy(out=hb[e, h][:], in_=mvv.rearrange("p t b -> p b t"))
+            else:
+                nc.vector.tensor_tensor(
+                    out=hb[e, h][:],
+                    in0=th[e, h][:].rearrange("p t b -> p b t"),
+                    in1=csb[:, e, :].unsqueeze(1).to_broadcast([P, 256, 4]),
+                    op=ALU.mult,
+                )
+
+        def h_quant(e, h):
+            nc.vector.quantize_mx(
+                out=hc[e, h][:].bitcast(FP8X4), scales=hs[e, h][:], in_=hb[e, h][:].rearrange("p b t -> p (b t)")
+            )
+
+        pairs = [(0, 0), (2, 0), (0, 1), (2, 1), (4, 0), (4, 1), (6, 0), (6, 1)]
+        N = len(pairs)
+        ys, sa, ot, qb = {}, {}, {}, {}
+
+        def y_mm(k):
+            i0, dh = pairs[k]
+            ys[k] = {}
+            for e in range(E):
+                for a in range(2):
+                    i = i0 + a
+                    h, li = i // 2, i % 2
+                    ys[k][e, a] = bank("y", 4, name="y")
+                    nc.tensor.matmul_mx(
+                        out=ys[k][e, a][:],
+                        lhsT=hc[e, h][:, li * P : (li + 1) * P].bitcast(FP8X4),
+                        lhsT_scale=hs[e, h][:, li * P : (li + 1) * P],
+                        rhs=uc[e, dh][:].bitcast(FP8X4),
+                        rhs_scale=us[e, dh][:],
+                        start=True,
+                        stop=True,
+                    )
+
+        def mix(k):
+            i0, dh = pairs[k]
+            sa[k] = [work.tile([P, 2, 512], F32, name=f"s{n}", tag=f"s{n}") for n in range(3)]
+            for a in range(2):
+                nc.vector.scalar_tensor_tensor(
+                    out=sa[k][0][:, a, :], in0=ys[k][0, a][:], scalar=gp[:, i0 + a, 0:1],
+                    in1=biasb[:, dh * 512 : (dh + 1) * 512], op0=ALU.mult, op1=ALU.add,
+                )
+            for a in range(2):
+                nc.vector.scalar_tensor_tensor(
+                    out=sa[k][1][:, a, :], in0=ys[k][1, a][:], scalar=gp[:, i0 + a, 1:2],
+                    in1=sa[k][0][:, a, :], op0=ALU.mult, op1=ALU.add,
+                )
+
+        def cross(k, which=(0, 1)):
+            i0, dh = pairs[k]
+            cols = slice(dh * 512, (dh + 1) * 512)
+            for a in which:
+                nc.vector.tensor_tensor(
+                    out=sa[k][2][:, a, :], in0=sa[k][1][:, a, :], in1=x0s[:, i0 + a, cols], op=ALU.mult
+                )
+
+        def resid(k, which=(0, 1)):
+            i0, dh = pairs[k]
+            if 0 in which:
+                ot[k] = work.tile([P, 2, 512], F32, name="ot", tag="ot", bufs=3)
+            gs = GS if k < N - 1 else 0
+            for a in which:
+                mine = max(0, gs - 512) if a == 0 else min(gs, 512)
+                split = 512 - mine
+                if split > 0:
+                    nc.vector.tensor_tensor(
+                        out=ot[k][:, a, :split], in0=sa[k][2][:, a, :split],
+                        in1=xs[:, i0 + a, dh * 512 : dh * 512 + split], op=ALU.add,
+                    )
+                if split < 512:
+                    nc.gpsimd.tensor_tensor(
+                        out=ot[k][:, a, split:], in0=sa[k][2][:, a, split:],
+                        in1=xs[:, i0 + a, dh * 512 + split : (dh + 1) * 512], op=ALU.add,
+                    )
+
+        def store_out(k, which=(0, 1)):
+            i0, dh = pairs[k]
+            lo, n = which[0], len(which)
+            nc.sync.dma_start(
+                out=out[(i0 + lo) * P : (i0 + lo + n) * P, dh * 512 : (dh + 1) * 512].rearrange("(i p) d -> p i d", p=P),
+                in_=ot[k][:, lo : lo + n, :],
+            )
+
+        def out_turn(k):
+            qb[k] = work.tile([P, 256, 4], BF16, name="qb", tag="qb", bufs=3, align_bytes=64)
+            for a in range(2):
+                tr = bank("tr", 2)
+                for t in range(4):
+                    nc.tensor.transpose(tr[:, t * P : (t + 1) * P], ot[k][:, a, t::4], idf[:])
+                nc.scalar.copy(out=qb[k][:, a * P : (a + 1) * P, :], in_=tr[:].rearrange("p (t r) -> p r t", t=4))
+
+        def out_quant(k):
+            i0, dh = pairs[k]
+            wq = work.tile([P, 256], U32, name="wq", tag="wq", bufs=3, align_bytes=64)
+            parts = 2 if k == N - 1 else 1
+            n = 256 // parts
+            for a in range(parts):
+                r0 = i0 * P + n * a
+                nc.vector.quantize_mx(
+                    out=wq[:, n * a : n * (a + 1)].bitcast(FP8X4), scales=osc[r0 // 512][:, dh, r0 % 512 : r0 % 512 + n],
+                    in_=qb[k][:, n * a : n * (a + 1), :].rearrange("p b t -> p (b t)"),
+                )
+                nc.sync.dma_start(
+                    out=words[dh, :, r0 : r0 + n, :].rearrange("p m t -> p (m t)").bitcast(I32),
+                    in_=wq[:, n * a : n * (a + 1)].bitcast(I32),
+                )
+
+        def store_scales(h):
+            cols = slice(512 * h, 512 * (h + 1))
+            for q in range(4):
+                nc.sync.dma_start(
+                    out=scales[:, 4 * q : 4 * q + 4, cols].rearrange("g q m -> q g m").bitcast(I32),
+                    in_=osc[h][32 * q : 32 * q + 4, :, :].bitcast(I32),
+                )
+
+        def bias_rows(dh):
+            bb = bank("aux", 2, name="bb")
+            nc.tensor.matmul(bb[:], lhsT=ones[:], rhs=bpad[:, dh * 512 : (dh + 1) * 512], start=True, stop=True)
+            nc.scalar.copy(out=biasb[:, dh * 512 : (dh + 1) * 512], in_=bb[:])
+
+        def gate_a():
+            nc.vector.tensor_tensor(out=gmx[:], in0=graw[:, :, 0], in1=graw[:, :, 1], op=ALU.max)
+            nc.gpsimd.tensor_tensor(
+                out=gd[:], in0=graw[:], in1=gmx[:].unsqueeze(2).to_broadcast([P, 8, E]), op=ALU.subtract
+            )
+            nc.scalar.activation(out=ge[:], in_=gd[:], func=ACT.Exp)
+            nc.gpsimd.tensor_tensor(out=gsum[:], in0=ge[:, :, 0], in1=ge[:, :, 1], op=ALU.add)
+
+        def gate_b():
+            nc.vector.reciprocal(out=grec[:], in_=gsum[:])
+            nc.gpsimd.tensor_tensor(out=gp[:], in0=ge[:], in1=grec[:].unsqueeze(2).to_broadcast([P, 8, E]), op=ALU.mult)
+
+        nc.gpsimd.tensor_copy(out=cf[:], in_=csb[:])
+        v_inter(0, 0)
+        x_turn(0)
+        x_turn(1)
+        v_quant(0, 0)
+        x_quant(0)
+        v_inter(0, 1)
+        v_inter(1, 0)
+        v_quant(0, 1)
+        v_quant(1, 0)
+        stage1(0, 0)
+        v_inter(1, 1)
+        bias_rows(0)
+        v_quant(1, 1)
+        stage1(1, 0)
+        h_mult(0, 0)
+        u_inter(0, 0)
+        x_turn(2)
+        x_turn(3)
+        u_inter(1, 0)
+        gate_a()
+        h_mult(1, 0)
+        h_quant(0, 0)
+        u_quant(0, 0)
+        gate_b()
+        h_quant(1, 0)
+        u_quant(1, 0)
+        y_mm(0)
+        x_quant(1)
+        stage1(0, 1)
+        bias_rows(1)
+        stage1(1, 1)
+
+        for k in range(N):
+            if k in (2, 4, 6):
+                y_mm(k + 1)
+            mix(k)
+            if k >= 1:
+                out_turn(k - 1)
+            if k >= 2:
+                out_quant(k - 2)
+            if k == 0:
+                h_mult(0, 1)
+                u_inter(0, 1)
+                h_mult(1, 1)
+                h_quant(0, 1)
+                x_turn(4)
+                x_turn(5)
+            if k == 1:
+                u_inter(1, 1)
+                u_quant(0, 1)
+                x_quant(2)
+                stage1(0, 2)
+                stage1(1, 2)
+            if k == 2:
+                h_mult(0, 2)
+                h_mult(1, 2)
+                x_turn(6)
+                x_turn(7)
+            if k == 3:
+                h_quant(0, 2)
+                h_quant(1, 2)
+                x_quant(3)
+                stage1(0, 3)
+                stage1(1, 3)
+            if k == 4:
+                h_mult(0, 3)
+                h_mult(1, 3)
+            if k == 5:
+                h_quant(0, 3)
+                h_quant(1, 3)
+            if k < N - 1:
+                cross(k)
+            else:
+                cross(k, (0,))
+                cross(k, (1,))
+                resid(k, (0,))
+                store_out(k, (0,))
+                resid(k, (1,))
+                store_out(k, (1,))
+            if k == 0:
+                h_quant(1, 1)
+            if k == 1:
+                u_quant(1, 1)
+            if k < N - 1:
+                resid(k)
+                store_out(k)
+            if k in (0, 1, 3, 5):
+                y_mm(k + 1)
+            if k == 5:
+                store_scales(0)
+        out_quant(N - 2)
+        out_turn(N - 1)
+        out_quant(N - 1)
+        store_scales(1)

@@ -16,11 +16,9 @@ ALU = mybir.AluOpType
 ACT = mybir.ActivationFunctionType
 P = 128
 
-GS = 768
-FORM3 = {(0, 2), (1, 2), (0, 3), (1, 3)}
-SSET = {}
-V_ROUTE = {(0, 0): "V", (0, 1): "V", (1, 0): "V", (1, 1): "PE"}
-U_ROUTE = {(0, 0): "PE", (1, 0): "PE", (0, 1): "S", (1, 1): "S"}
+YB, AUXB, TRB = 4, 2, 2
+GSP = {k: (256, 512) for k in range(7)}
+GSP[7] = (0, 0)
 
 
 def tile_dcnv2lowrankexpertcross_x1_kernel(tc, x0, x, v, c, u, bias, gate, out, words, scales):
@@ -29,6 +27,7 @@ def tile_dcnv2lowrankexpertcross_x1_kernel(tc, x0, x, v, c, u, bias, gate, out, 
         keep = ctx.enter_context(tc.tile_pool(name="keep", bufs=1))
         work = ctx.enter_context(tc.tile_pool(name="work", bufs=2))
         psum = ctx.enter_context(tc.psum_pool(name="psum", bufs=1))
+        ctx.enter_context(tc.manual_schedule())
 
         xs = keep.tile([P, 8, D], BF16, name="xs", align_bytes=64)
         x0s = keep.tile([P, 8, D], BF16, name="x0s", align_bytes=64)
@@ -66,6 +65,8 @@ def tile_dcnv2lowrankexpertcross_x1_kernel(tc, x0, x, v, c, u, bias, gate, out, 
         idb = keep.tile([P, P], BF16, name="idb")
         warm = keep.tile([P, 8], F32, name="warm")
 
+        TB = {"y": YB, "aux": AUXB, "tr": TRB}
+
         def bank(tag, bufs, dtype=F32, name=None):
             return psum.tile([P, 512 if dtype == F32 else 1024], dtype, name=name or tag, tag=tag, bufs=bufs)
 
@@ -88,44 +89,36 @@ def tile_dcnv2lowrankexpertcross_x1_kernel(tc, x0, x, v, c, u, bias, gate, out, 
         nc.gpsimd.memset(bpad[:], 0.0)
         nc.scalar.activation(out=warm[:], in_=warm[:], func=ACT.Tanh)
 
-        for q in range(2):
+        def load_v0(q):
             cols = slice(256 * q, 256 * (q + 1))
             nc.sync.dma_start(
                 out=vraw[0, 0][:, :, cols], in_=v[0, :512, cols].rearrange("(p j) w -> p j w", j=4)
             )
-        load_x(xs, x, 0)
-        load_x(xs, x, 1)
-        load_v(0, 1)
-        nc.sync.dma_start(out=csb[:], in_=c.rearrange("e (p t) -> p e t", t=4))
-        nc.sync.dma_start(out=bpad[0:1, :], in_=bias.unsqueeze(0))
-        load_v(1, 0)
-        load_v(1, 1)
-        load_u(0, 0)
-        nc.sync.dma_start(out=graw[:], in_=gate.rearrange("(i p) e -> p i e", p=P))
-        load_u(1, 0)
-        load_x(xs, x, 2)
-        load_x(xs, x, 3)
-        load_x(x0s, x0, 0)
-        load_x(x0s, x0, 1)
-        load_u(0, 1)
-        load_u(1, 1)
-        for i in (2, 3):
-            load_x(x0s, x0, i)
-        for i in range(4, 8):
-            load_x(xs, x, i)
-        for i in range(4, 8):
-            load_x(x0s, x0, i)
+
+        def load_bias():
+            nc.sync.dma_start(out=bpad[0:1, :], in_=bias.unsqueeze(0))
+
+        def load_c():
+            nc.sync.dma_start(out=csb[:], in_=c.rearrange("e (p t) -> p e t", t=4))
+
+        def load_gate():
+            nc.sync.dma_start(out=graw[:], in_=gate.rearrange("(i p) e -> p i e", p=P))
+
+        xtr = {}
 
         def x_turn(i):
-            tr = bank("tr", 2)
+            tr = bank("tr", TB["tr"])
             trv = tr[:].rearrange("p (g u r) -> p g u r", g=2, u=2)
             xw = xs[:, i, :].bitcast(F32)
             for g in range(2):
                 for w in range(2):
                     nc.tensor.transpose(trv[:, g, w, :], xw[:, 256 * g + w : 256 * (g + 1) : 2], idf[:])
+            xtr[i] = tr
+
+        def x_evac(i):
             li = i % 2
             nc.scalar.copy(
-                out=xg[i // 2][:, :, li * P : (li + 1) * P, :], in_=tr[:].rearrange("p (g u r) -> p g r u", g=2, u=2)
+                out=xg[i // 2][:, :, li * P : (li + 1) * P, :], in_=xtr[i][:].rearrange("p (g u r) -> p g r u", g=2, u=2)
             )
 
         def x_quant(h):
@@ -135,90 +128,95 @@ def tile_dcnv2lowrankexpertcross_x1_kernel(tc, x0, x, v, c, u, bias, gate, out, 
                 in_=xg[h][:].rearrange("p g b u -> p (g b u)").bitcast(BF16),
             )
 
-        TB = {"y": 4, "aux": 2, "tr": 2}
+        mvs = {}
 
-        def interleave(route, raw, dst_half, pat, tag):
-            for q in range(2):
-                cols = slice(256 * q, 256 * (q + 1))
-                if route == "PE":
-                    mv = bank(tag, TB[tag], BF16, name="mv")
-                    mvv = mv[:].rearrange("p (j c) -> p j c", j=4)
-                    for k in range(2):
-                        nc.tensor.matmul(
-                            mvv[:, 2 * k : 2 * k + 2, :], lhsT=idb[:], rhs=raw[:, 2 * k : 2 * k + 2, cols], start=True, stop=True
-                        )
-                    nc.scalar.copy(out=dst_half(q), in_=mvv.rearrange(pat[0], **pat[1]))
-                elif route == "S":
-                    nc.scalar.copy(out=dst_half(q), in_=raw[:, :, cols].rearrange(pat[0], **pat[1]))
-                else:
-                    nc.vector.tensor_copy(out=dst_half(q), in_=raw[:, :, cols].rearrange(pat[0], **pat[1]))
+        def move(tag, key, rows):
+            mv = bank(tag, TB[tag], BF16, name="mv")
+            mvs[key] = mv[:].rearrange("p (j c) -> p j c", j=4)
+            for k in range(2):
+                nc.tensor.matmul(
+                    mvs[key][:, 2 * k : 2 * k + 2, :], lhsT=idb[:], rhs=rows[:, 2 * k : 2 * k + 2, :], start=True, stop=True
+                )
 
-        def v_inter(e, g):
-            dst = vg[e, g][:].rearrange("p (t m j) -> p t m j", t=4, j=4)
-            interleave(
-                V_ROUTE[e, g], vraw[e, g], lambda q: dst[:, :, 64 * q : 64 * (q + 1), :], ("p j (m t) -> p t m j", {"t": 4}), "y"
+        def vdst(e, g, q):
+            return vg[e, g][:].rearrange("p (t m j) -> p t m j", t=4, j=4)[:, :, 64 * q : 64 * (q + 1), :]
+
+        def v_inter(e, g, q):
+            nc.vector.tensor_copy(
+                out=vdst(e, g, q), in_=vraw[e, g][:, :, 256 * q : 256 * (q + 1)].rearrange("p j (m t) -> p t m j", t=4)
             )
+
+        def v_move(e, g, q, tag="y"):
+            move(tag, ("v", e, g, q), vraw[e, g][:, :, 256 * q : 256 * (q + 1)])
+
+        def v_evac(e, g, q):
+            nc.scalar.copy(out=vdst(e, g, q), in_=mvs["v", e, g, q].rearrange("p j (m t) -> p t m j", t=4))
 
         def v_quant(e, g):
             nc.vector.quantize_mx(out=vc[e, g][:].bitcast(FP8X4), scales=vs[e, g][:], in_=vg[e, g][:])
 
-        def u_inter(e, dh):
-            interleave(
-                U_ROUTE[e, dh], uraw[e, dh], lambda q: ug[e, dh][:, 256 * q : 256 * (q + 1), :], ("p j c -> p c j", {}), "y" if dh == 0 else "aux"
-            )
+        def u_move(e, dh, q, tag="y"):
+            move(tag, ("u", e, dh, q), uraw[e, dh][:, :, 256 * q : 256 * (q + 1)])
+
+        def u_evac(e, dh, q):
+            nc.scalar.copy(out=ug[e, dh][:, 256 * q : 256 * (q + 1), :], in_=mvs["u", e, dh, q].rearrange("p j c -> p c j"))
+
+        def u_inter(e, dh, q):
+            cols = slice(256 * q, 256 * (q + 1))
+            nc.scalar.copy(out=ug[e, dh][:, cols, :], in_=uraw[e, dh][:, :, cols].rearrange("p j c -> p c j"))
 
         def u_quant(e, dh):
             nc.vector.quantize_mx(
                 out=uc[e, dh][:].bitcast(FP8X4), scales=us[e, dh][:], in_=ug[e, dh][:].rearrange("p c j -> p (c j)")
             )
 
-        th = {}
+        th, acc1, hb, ht = {}, {}, {}, {}
 
-        def stage1(e, h):
-            th[e, h] = work.tile([P, 4, 256], F32, name="th", tag="th", bufs=4)
-            for q in range(2):
-                acc = bank("aux", 2, name="a1")
-                for k in range(2):
-                    t = 2 * q + k
-                    for g in range(2):
-                        nc.tensor.matmul_mx(
-                            out=acc[:, 256 * k : 256 * (k + 1)],
-                            lhsT=vc[e, g][:, t * P : (t + 1) * P].bitcast(FP8X4),
-                            lhsT_scale=vs[e, g][:, t * P : (t + 1) * P],
-                            rhs=xc[h][:, g, :].bitcast(FP8X4),
-                            rhs_scale=xsc[h][:, g, :],
-                            start=(g == 0),
-                            stop=(g == 1),
-                        )
-                nc.scalar.activation(
-                    out=th[e, h][:, 2 * q : 2 * q + 2, :].rearrange("p t b -> p (t b)"), in_=acc[:], func=ACT.Tanh
-                )
+        def stage1(e, h, q):
+            acc1[e, h, q] = bank("aux", TB["aux"], name="a1")
+            for k in range(2):
+                t = 2 * q + k
+                for g in range(2):
+                    nc.tensor.matmul_mx(
+                        out=acc1[e, h, q][:, 256 * k : 256 * (k + 1)],
+                        lhsT=vc[e, g][:, t * P : (t + 1) * P].bitcast(FP8X4),
+                        lhsT_scale=vs[e, g][:, t * P : (t + 1) * P],
+                        rhs=xc[h][:, g, :].bitcast(FP8X4),
+                        rhs_scale=xsc[h][:, g, :],
+                        start=(g == 0),
+                        stop=(g == 1),
+                    )
 
-        hb = {}
+        def tanh(e, h, q):
+            if q == 0:
+                th[e, h] = work.tile([P, 4, 256], F32, name="th", tag="th", bufs=4)
+            nc.scalar.activation(
+                out=th[e, h][:, 2 * q : 2 * q + 2, :].rearrange("p t b -> p (t b)"), in_=acc1[e, h, q][:], func=ACT.Tanh
+            )
+
+        def new_hb(e, h):
+            hb[e, h] = work.tile([P, 256, 4], BF16, name="hb", tag="hb", bufs=3, align_bytes=64)
 
         def h_mult(e, h):
-            hb[e, h] = work.tile([P, 256, 4], BF16, name="hb", tag="hb", bufs=3, align_bytes=64)
-            if (e, h) in FORM3 or (e, h) in SSET:
-                ht = work.tile([P, 4, 256], BF16, name="ht", tag="ht")
-                for t in range(4):
-                    nc.scalar.activation(out=ht[:, t, :], in_=th[e, h][:, t, :], func=ACT.Copy, scale=cf[:, e, t : t + 1])
-                if (e, h) in SSET:
-                    nc.scalar.copy(out=hb[e, h][:], in_=ht[:].rearrange("p t b -> p b t"))
-                else:
-                    mv = bank("aux", 2, BF16, name="mv")
-                    mvv = mv[:].rearrange("p (t b) -> p t b", t=4)
-                    for k in range(2):
-                        nc.tensor.matmul(
-                            mvv[:, 2 * k : 2 * k + 2, :], lhsT=idb[:], rhs=ht[:, 2 * k : 2 * k + 2, :], start=True, stop=True
-                        )
-                    nc.scalar.copy(out=hb[e, h][:], in_=mvv.rearrange("p t b -> p b t"))
-            else:
-                nc.vector.tensor_tensor(
-                    out=hb[e, h][:],
-                    in0=th[e, h][:].rearrange("p t b -> p b t"),
-                    in1=csb[:, e, :].unsqueeze(1).to_broadcast([P, 256, 4]),
-                    op=ALU.mult,
-                )
+            new_hb(e, h)
+            nc.vector.tensor_tensor(
+                out=hb[e, h][:],
+                in0=th[e, h][:].rearrange("p t b -> p b t"),
+                in1=csb[:, e, :].unsqueeze(1).to_broadcast([P, 256, 4]),
+                op=ALU.mult,
+            )
+
+        def h_scale(e, h):
+            ht[e, h] = work.tile([P, 4, 256], BF16, name="ht", tag="ht")
+            for t in range(4):
+                nc.scalar.activation(out=ht[e, h][:, t, :], in_=th[e, h][:, t, :], func=ACT.Copy, scale=cf[:, e, t : t + 1])
+
+        def h_move(e, h):
+            move("aux", ("h", e, h), ht[e, h])
+
+        def h_evac(e, h):
+            new_hb(e, h)
+            nc.scalar.copy(out=hb[e, h][:], in_=mvs["h", e, h].rearrange("p t b -> p b t"))
 
         def h_quant(e, h):
             nc.vector.quantize_mx(
@@ -229,16 +227,15 @@ def tile_dcnv2lowrankexpertcross_x1_kernel(tc, x0, x, v, c, u, bias, gate, out, 
         N = len(pairs)
         ys, sa, ot, qb = {}, {}, {}, {}
 
-        def y_mm(k):
+        def y_mm(k, e):
             i0, dh = pairs[k]
-            ys[k] = {}
-            for e in range(E):
+            if True:
                 for a in range(2):
                     i = i0 + a
                     h, li = i // 2, i % 2
-                    ys[k][e, a] = bank("y", 4, name="y")
+                    ys[k, e, a] = bank("y", TB["y"], name="y")
                     nc.tensor.matmul_mx(
-                        out=ys[k][e, a][:],
+                        out=ys[k, e, a][:],
                         lhsT=hc[e, h][:, li * P : (li + 1) * P].bitcast(FP8X4),
                         lhsT_scale=hs[e, h][:, li * P : (li + 1) * P],
                         rhs=uc[e, dh][:].bitcast(FP8X4),
@@ -247,46 +244,44 @@ def tile_dcnv2lowrankexpertcross_x1_kernel(tc, x0, x, v, c, u, bias, gate, out, 
                         stop=True,
                     )
 
-        def mix(k):
+        def mix0(k, a):
             i0, dh = pairs[k]
-            sa[k] = [work.tile([P, 2, 512], F32, name=f"s{n}", tag=f"s{n}") for n in range(3)]
-            for a in range(2):
-                nc.vector.scalar_tensor_tensor(
-                    out=sa[k][0][:, a, :], in0=ys[k][0, a][:], scalar=gp[:, i0 + a, 0:1],
-                    in1=biasb[:, dh * 512 : (dh + 1) * 512], op0=ALU.mult, op1=ALU.add,
-                )
-            for a in range(2):
-                nc.vector.scalar_tensor_tensor(
-                    out=sa[k][1][:, a, :], in0=ys[k][1, a][:], scalar=gp[:, i0 + a, 1:2],
-                    in1=sa[k][0][:, a, :], op0=ALU.mult, op1=ALU.add,
-                )
+            if a == 0:
+                sa[k] = [work.tile([P, 2, 512], F32, name=f"s{n}", tag=f"s{n}") for n in range(3)]
+            nc.vector.scalar_tensor_tensor(
+                out=sa[k][0][:, a, :], in0=ys[k, 0, a][:], scalar=gp[:, i0 + a, 0:1],
+                in1=biasb[:, dh * 512 : (dh + 1) * 512], op0=ALU.mult, op1=ALU.add,
+            )
 
-        def cross(k, which=(0, 1)):
+        def mix1(k, a):
+            i0, dh = pairs[k]
+            nc.vector.scalar_tensor_tensor(
+                out=sa[k][1][:, a, :], in0=ys[k, 1, a][:], scalar=gp[:, i0 + a, 1:2],
+                in1=sa[k][0][:, a, :], op0=ALU.mult, op1=ALU.add,
+            )
+
+        def cross(k, a):
             i0, dh = pairs[k]
             cols = slice(dh * 512, (dh + 1) * 512)
-            for a in which:
-                nc.vector.tensor_tensor(
-                    out=sa[k][2][:, a, :], in0=sa[k][1][:, a, :], in1=x0s[:, i0 + a, cols], op=ALU.mult
-                )
-
-        def resid(k, which=(0, 1)):
-            i0, dh = pairs[k]
-            if 0 in which:
+            nc.vector.tensor_tensor(out=sa[k][2][:, a, :], in0=sa[k][1][:, a, :], in1=x0s[:, i0 + a, cols], op=ALU.mult)
+            if a == 0:
                 ot[k] = work.tile([P, 2, 512], F32, name="ot", tag="ot", bufs=3)
-            gs = GS if k < N - 1 else 0
-            for a in which:
-                mine = max(0, gs - 512) if a == 0 else min(gs, 512)
-                split = 512 - mine
-                if split > 0:
-                    nc.vector.tensor_tensor(
-                        out=ot[k][:, a, :split], in0=sa[k][2][:, a, :split],
-                        in1=xs[:, i0 + a, dh * 512 : dh * 512 + split], op=ALU.add,
-                    )
-                if split < 512:
-                    nc.gpsimd.tensor_tensor(
-                        out=ot[k][:, a, split:], in0=sa[k][2][:, a, split:],
-                        in1=xs[:, i0 + a, dh * 512 + split : (dh + 1) * 512], op=ALU.add,
-                    )
+
+        def add_x(eng, k, a, lo, hi):
+            i0, dh = pairs[k]
+            eng.tensor_tensor(
+                out=ot[k][:, a, lo:hi], in0=sa[k][2][:, a, lo:hi], in1=xs[:, i0 + a, dh * 512 + lo : dh * 512 + hi], op=ALU.add
+            )
+
+        def resid_v(k, a):
+            split = 512 - GSP[k][a]
+            if split > 0:
+                add_x(nc.vector, k, a, 0, split)
+
+        def resid_g(k, a):
+            split = 512 - GSP[k][a]
+            if split < 512:
+                add_x(nc.gpsimd, k, a, split, 512)
 
         def store_out(k, which=(0, 1)):
             i0, dh = pairs[k]
@@ -296,20 +291,31 @@ def tile_dcnv2lowrankexpertcross_x1_kernel(tc, x0, x, v, c, u, bias, gate, out, 
                 in_=ot[k][:, lo : lo + n, :],
             )
 
-        def out_turn(k):
-            qb[k] = work.tile([P, 256, 4], BF16, name="qb", tag="qb", bufs=3, align_bytes=64)
-            for a in range(2):
-                tr = bank("tr", 2)
+        otr = {}
+
+        def out_turn(k, a):
+            if True:
+                tr = bank("tr", TB["tr"])
                 for t in range(4):
                     nc.tensor.transpose(tr[:, t * P : (t + 1) * P], ot[k][:, a, t::4], idf[:])
-                nc.scalar.copy(out=qb[k][:, a * P : (a + 1) * P, :], in_=tr[:].rearrange("p (t r) -> p r t", t=4))
+                otr[k, a] = tr
 
-        def out_quant(k):
+        def out_evac(k, a):
+            if a == 0:
+                qb[k] = work.tile([P, 256, 4], BF16, name="qb", tag="qb", bufs=3, align_bytes=64)
+            if True:
+                nc.scalar.copy(out=qb[k][:, a * P : (a + 1) * P, :], in_=otr[k, a][:].rearrange("p (t r) -> p r t", t=4))
+
+        wqs = {}
+
+        def out_quant(k, a=0):
             i0, dh = pairs[k]
-            wq = work.tile([P, 256], U32, name="wq", tag="wq", bufs=3, align_bytes=64)
+            if a == 0:
+                wqs[k] = work.tile([P, 256], U32, name="wq", tag="wq", bufs=3, align_bytes=64)
+            wq = wqs[k]
             parts = 2 if k == N - 1 else 1
             n = 256 // parts
-            for a in range(parts):
+            if True:
                 r0 = i0 * P + n * a
                 nc.vector.quantize_mx(
                     out=wq[:, n * a : n * (a + 1)].bitcast(FP8X4), scales=osc[r0 // 512][:, dh, r0 % 512 : r0 % 512 + n],
@@ -328,115 +334,335 @@ def tile_dcnv2lowrankexpertcross_x1_kernel(tc, x0, x, v, c, u, bias, gate, out, 
                     in_=osc[h][32 * q : 32 * q + 4, :, :].bitcast(I32),
                 )
 
-        def bias_rows(dh):
-            bb = bank("aux", 2, name="bb")
-            nc.tensor.matmul(bb[:], lhsT=ones[:], rhs=bpad[:, dh * 512 : (dh + 1) * 512], start=True, stop=True)
-            nc.scalar.copy(out=biasb[:, dh * 512 : (dh + 1) * 512], in_=bb[:])
+        bbs = {}
 
-        def gate_a():
+        def bias_mm(dh):
+            bbs[dh] = bank("aux", TB["aux"], name="bb")
+            nc.tensor.matmul(bbs[dh][:], lhsT=ones[:], rhs=bpad[:, dh * 512 : (dh + 1) * 512], start=True, stop=True)
+
+        def bias_evac(dh):
+            nc.scalar.copy(out=biasb[:, dh * 512 : (dh + 1) * 512], in_=bbs[dh][:])
+
+        def gate1():
             nc.vector.tensor_tensor(out=gmx[:], in0=graw[:, :, 0], in1=graw[:, :, 1], op=ALU.max)
+
+        def gate2():
             nc.gpsimd.tensor_tensor(
                 out=gd[:], in0=graw[:], in1=gmx[:].unsqueeze(2).to_broadcast([P, 8, E]), op=ALU.subtract
             )
+
+        def gate3():
             nc.scalar.activation(out=ge[:], in_=gd[:], func=ACT.Exp)
+
+        def gate4():
             nc.gpsimd.tensor_tensor(out=gsum[:], in0=ge[:, :, 0], in1=ge[:, :, 1], op=ALU.add)
 
-        def gate_b():
+        def gate5():
             nc.vector.reciprocal(out=grec[:], in_=gsum[:])
+
+        def gate6():
             nc.gpsimd.tensor_tensor(out=gp[:], in0=ge[:], in1=grec[:].unsqueeze(2).to_broadcast([P, 8, E]), op=ALU.mult)
 
-        nc.gpsimd.tensor_copy(out=cf[:], in_=csb[:])
-        v_inter(0, 0)
-        x_turn(0)
-        x_turn(1)
-        v_quant(0, 0)
-        x_quant(0)
-        v_inter(0, 1)
-        v_inter(1, 0)
-        v_quant(0, 1)
-        v_quant(1, 0)
-        stage1(0, 0)
-        v_inter(1, 1)
-        bias_rows(0)
-        v_quant(1, 1)
-        stage1(1, 0)
-        h_mult(0, 0)
-        u_inter(0, 0)
-        x_turn(2)
-        x_turn(3)
-        u_inter(1, 0)
-        gate_a()
-        h_mult(1, 0)
-        h_quant(0, 0)
-        u_quant(0, 0)
-        gate_b()
-        h_quant(1, 0)
-        u_quant(1, 0)
-        y_mm(0)
-        x_quant(1)
-        stage1(0, 1)
-        bias_rows(1)
-        stage1(1, 1)
+        def cf_copy():
+            nc.gpsimd.tensor_copy(out=cf[:], in_=csb[:])
 
-        for k in range(N):
-            if k in (2, 4, 6):
-                y_mm(k + 1)
-            mix(k)
-            if k >= 1:
-                out_turn(k - 1)
-            if k >= 2:
-                out_quant(k - 2)
-            if k == 0:
-                h_mult(0, 1)
-                u_inter(0, 1)
-                h_mult(1, 1)
-                h_quant(0, 1)
-                x_turn(4)
-                x_turn(5)
-            if k == 1:
-                u_inter(1, 1)
-                u_quant(0, 1)
-                x_quant(2)
-                stage1(0, 2)
-                stage1(1, 2)
-            if k == 2:
-                h_mult(0, 2)
-                h_mult(1, 2)
-                x_turn(6)
-                x_turn(7)
-            if k == 3:
-                h_quant(0, 2)
-                h_quant(1, 2)
-                x_quant(3)
-                stage1(0, 3)
-                stage1(1, 3)
-            if k == 4:
-                h_mult(0, 3)
-                h_mult(1, 3)
-            if k == 5:
-                h_quant(0, 3)
-                h_quant(1, 3)
-            if k < N - 1:
-                cross(k)
-            else:
-                cross(k, (0,))
-                cross(k, (1,))
-                resid(k, (0,))
-                store_out(k, (0,))
-                resid(k, (1,))
-                store_out(k, (1,))
-            if k == 0:
-                h_quant(1, 1)
-            if k == 1:
-                u_quant(1, 1)
-            if k < N - 1:
-                resid(k)
-                store_out(k)
-            if k in (0, 1, 3, 5):
-                y_mm(k + 1)
-            if k == 5:
-                store_scales(0)
-        out_quant(N - 2)
-        out_turn(N - 1)
-        out_quant(N - 1)
+        def h_mult_g(e, h):
+            new_hb(e, h)
+            nc.gpsimd.tensor_tensor(
+                out=hb[e, h][:],
+                in0=th[e, h][:].rearrange("p t b -> p b t"),
+                in1=csb[:, e, :].unsqueeze(1).to_broadcast([P, 256, 4]),
+                op=ALU.mult,
+            )
+
+        load_v0(0)
+        load_gate()
+        load_v(0, 1)
+        load_x(xs, x, 0)
+        x_turn(0)
+        load_x(xs, x, 1)
+        load_bias()
+        x_evac(0)
+        bias_mm(0)
+        gate1()
+        v_inter(0, 0, 0)
+        bias_mm(1)
+        x_turn(1)
+        v_inter(0, 1, 0)
+        load_v0(1)
+        load_v(1, 0)
+        v_move(1, 0, 0)
+        load_v(1, 1)
+        bias_evac(0)
+        gate2()
+        x_evac(1)
+        gate3()
+        load_u(0, 0)
+        v_inter(0, 1, 1)
+        bias_evac(1)
+        gate4()
+        v_evac(1, 0, 0)
+        v_move(1, 0, 1)
+        v_quant(0, 1)
+        v_evac(1, 0, 1)
+        v_move(1, 1, 0)
+        load_u(1, 0)
+        v_move(1, 1, 1)
+        v_evac(1, 1, 0)
+        u_move(0, 0, 0)
+        v_inter(0, 0, 1)
+        load_c()
+        v_evac(1, 1, 1)
+        load_x(xs, x, 2)
+        v_quant(0, 0)
+        load_x(xs, x, 3)
+        x_quant(0)
+        stage1(0, 0, 0)
+        stage1(0, 0, 1)
+        gate5()
+        v_quant(1, 0)
+        u_evac(0, 0, 0)
+        tanh(0, 0, 0)
+        tanh(0, 0, 1)
+        v_quant(1, 1)
+        u_move(0, 0, 1)
+        load_x(x0s, x0, 0)
+        stage1(1, 0, 0)
+        stage1(1, 0, 1)
+        u_move(1, 0, 0)
+        load_x(xs, x, 4)
+        h_mult(0, 0)
+        u_evac(0, 0, 1)
+        u_quant(0, 0)
+        h_quant(0, 0)
+        load_u(1, 1)
+        load_x(x0s, x0, 2)
+        u_move(1, 0, 1)
+        gate6()
+        tanh(1, 0, 0)
+        tanh(1, 0, 1)
+        x_turn(2)
+        u_evac(1, 0, 0)
+        x_turn(3)
+        h_mult(1, 0)
+        y_mm(0, 0)
+        load_u(0, 1)
+        u_evac(1, 0, 1)
+        load_x(xs, x, 6)
+        x_evac(2)
+        load_x(x0s, x0, 1)
+        x_turn(4)
+        u_quant(1, 0)
+        x_evac(3)
+        h_quant(1, 0)
+        mix0(0, 0)
+        resid_v(3, 1)
+        y_mm(0, 1)
+        mix0(0, 1)
+        load_x(xs, x, 5)
+        u_inter(0, 1, 0)
+        x_evac(4)
+        x_quant(1)
+        u_inter(0, 1, 1)
+        x_turn(5)
+        stage1(0, 1, 0)
+        tanh(0, 1, 0)
+        stage1(0, 1, 1)
+        tanh(0, 1, 1)
+        x_turn(6)
+        load_x(xs, x, 7)
+        x_evac(5)
+        mix1(0, 0)
+        stage1(1, 1, 0)
+        mix1(0, 1)
+        tanh(1, 1, 0)
+        cross(0, 0)
+        cross(0, 1)
+        stage1(1, 1, 1)
+        resid_v(0, 0)
+        u_quant(0, 1)
+        tanh(1, 1, 1)
+        x_turn(7)
+        h_mult(0, 1)
+        x_quant(2)
+        load_x(x0s, x0, 5)
+        u_inter(1, 1, 0)
+        h_quant(0, 1)
+        x_evac(6)
+        h_mult(1, 1)
+        cf_copy()
+        stage1(1, 2, 0)
+        y_mm(1, 0)
+        resid_v(2, 1)
+        mix0(1, 0)
+        load_x(x0s, x0, 3)
+        h_quant(1, 1)
+        stage1(0, 2, 0)
+        tanh(0, 2, 0)
+        resid_g(0, 1)
+        y_mm(3, 0)
+        mix0(1, 1)
+        mix0(3, 0)
+        y_mm(1, 1)
+        mix1(1, 0)
+        mix0(3, 1)
+        mix1(1, 1)
+        tanh(1, 2, 0)
+        resid_g(0, 0)
+        u_inter(1, 1, 1)
+        stage1(1, 2, 1)
+        load_x(x0s, x0, 6)
+        x_evac(7)
+        tanh(1, 2, 1)
+        cross(1, 0)
+        load_x(x0s, x0, 4)
+        out_turn(0, 0)
+        h_scale(1, 2)
+        u_quant(1, 1)
+        stage1(0, 2, 1)
+        resid_v(0, 1)
+        x_quant(3)
+        y_mm(2, 0)
+        mix0(2, 0)
+        cross(1, 1)
+        h_move(1, 2)
+        tanh(0, 2, 1)
+        mix0(2, 1)
+        h_evac(1, 2)
+        y_mm(2, 1)
+        out_turn(0, 1)
+        stage1(0, 3, 0)
+        resid_v(1, 0)
+        store_out(0)
+        out_evac(0, 0)
+        mix1(2, 0)
+        mix1(2, 1)
+        out_evac(0, 1)
+        h_quant(1, 2)
+        resid_v(4, 1)
+        y_mm(3, 1)
+        cross(2, 0)
+        resid_g(1, 0)
+        resid_g(1, 1)
+        mix1(3, 0)
+        h_mult(0, 2)
+        resid_v(2, 0)
+        out_turn(1, 0)
+        stage1(1, 3, 0)
+        out_turn(1, 1)
+        tanh(0, 3, 0)
+        tanh(1, 3, 0)
+        stage1(1, 3, 1)
+        out_evac(1, 0)
+        cross(3, 0)
+        resid_v(6, 1)
+        h_quant(0, 2)
+        resid_v(5, 1)
+        y_mm(4, 0)
+        mix1(3, 1)
+        out_quant(0)
+        mix0(4, 0)
+        resid_v(3, 0)
+        y_mm(5, 0)
+        cross(2, 1)
+        resid_g(3, 0)
+        stage1(0, 3, 1)
+        out_evac(1, 1)
+        tanh(1, 3, 1)
+        mix0(4, 1)
+        h_scale(1, 3)
+        tanh(0, 3, 1)
+        resid_g(2, 0)
+        h_scale(0, 3)
+        store_out(1)
+        out_quant(1)
+        cross(3, 1)
+        y_mm(4, 1)
+        h_move(1, 3)
+        h_evac(1, 3)
+        resid_g(2, 1)
+        mix1(4, 0)
+        h_move(0, 3)
+        mix0(5, 0)
+        resid_g(3, 1)
+        h_evac(0, 3)
+        mix0(5, 1)
+        h_quant(1, 3)
+        mix1(4, 1)
+        y_mm(5, 1)
+        h_quant(0, 3)
+        out_turn(3, 0)
+        cross(4, 0)
+        store_out(2)
+        store_out(3)
+        out_evac(3, 0)
+        out_turn(2, 0)
+        out_turn(3, 1)
+        mix1(5, 0)
+        y_mm(6, 0)
+        out_evac(2, 0)
+        out_evac(3, 1)
+        resid_v(4, 0)
+        out_turn(2, 1)
+        mix1(5, 1)
+        cross(4, 1)
+        out_evac(2, 1)
+        resid_g(4, 0)
+        cross(5, 0)
+        mix0(6, 0)
+        load_x(x0s, x0, 7)
+        out_quant(3)
+        resid_v(5, 0)
+        y_mm(6, 1)
+        out_quant(2)
+        mix1(6, 0)
+        mix0(6, 1)
+        cross(5, 1)
+        mix1(6, 1)
+        resid_g(4, 1)
+        cross(6, 0)
+        y_mm(7, 0)
+        store_out(4)
+        cross(6, 1)
+        mix0(7, 0)
+        y_mm(7, 1)
+        out_turn(4, 0)
+        resid_g(5, 0)
+        store_scales(0)
+        resid_v(6, 0)
+        out_turn(4, 1)
+        out_evac(4, 0)
+        mix1(7, 0)
+        mix0(7, 1)
+        out_turn(5, 0)
+        resid_g(5, 1)
+        out_evac(4, 1)
+        cross(7, 0)
+        mix1(7, 1)
+        out_evac(5, 0)
+        store_out(5)
+        out_turn(5, 1)
+        out_evac(5, 1)
+        resid_v(7, 0)
+        resid_g(6, 1)
+        resid_g(6, 0)
+        out_turn(6, 0)
+        store_out(6)
+        out_evac(6, 0)
+        out_quant(4)
+        cross(7, 1)
+        store_out(7, (0,))
+        out_quant(5)
+        out_turn(7, 0)
+        resid_v(1, 1)
+        out_evac(7, 0)
+        out_turn(6, 1)
+        resid_v(7, 1)
+        store_out(7, (1,))
+        out_turn(7, 1)
+        out_evac(6, 1)
+        out_quant(6)
+        out_quant(7)
+        out_evac(7, 1)
+        out_quant(7, 1)
         store_scales(1)

@@ -36,13 +36,17 @@ def tile_dcnv2lowrankexpertcross_x1_kernel(tc, x0, x, v, c, u, bias, gate, out, 
         for e in range(E):
             for g in range(2):
                 vraw[e, g] = keep.tile([P, 4, R], BF16, name=f"vraw{e}{g}", align_bytes=64)
-                vg[e, g] = keep.tile([P, 4 * R], BF16, name=f"vg{e}{g}", align_bytes=64)
                 vc[e, g] = keep.tile([P, R], U32, name=f"vc{e}{g}", align_bytes=64)
                 vs[e, g] = keep.tile([P, R], U8, name=f"vs{e}{g}", align_bytes=64)
                 uraw[e, g] = keep.tile([P, 4, 512], BF16, name=f"uraw{e}{g}", align_bytes=64)
-                ug[e, g] = keep.tile([P, 512, 4], BF16, name=f"ug{e}{g}", align_bytes=64)
                 uc[e, g] = keep.tile([P, 512], U32, name=f"uc{e}{g}", align_bytes=64)
                 us[e, g] = keep.tile([P, 512], U8, name=f"us{e}{g}", align_bytes=64)
+        for e in range(E):
+            for g in range(2):
+                vg[e, g] = keep.tile([P, 4 * R], BF16, name=f"vg{e}{g}", tag="grouped", bufs=6, align_bytes=64)
+        for dh in range(2):
+            for e in range(E):
+                ug[e, dh] = keep.tile([P, 512, 4], BF16, name=f"ug{e}{dh}", tag="grouped", bufs=6, align_bytes=64)
         xg = [keep.tile([P, 2, 256, 2], F32, name=f"xg{h}", align_bytes=64) for h in range(4)]
         xc = [keep.tile([P, 2, 256], U32, name=f"xc{h}", align_bytes=64) for h in range(4)]
         xsc = [keep.tile([P, 2, 256], U8, name=f"xsc{h}", align_bytes=64) for h in range(4)]
@@ -51,6 +55,7 @@ def tile_dcnv2lowrankexpertcross_x1_kernel(tc, x0, x, v, c, u, bias, gate, out, 
         osc = [keep.tile([P, 2, 512], U8, name=f"osc{h}", align_bytes=64) for h in range(2)]
         cf = keep.tile([P, E, 4], F32, name="cf")
         csb = keep.tile([P, E, 4], BF16, name="csb")
+        pad = keep.tile([P, 768], BF16, name="pad")
         graw = keep.tile([P, 8, E], BF16, name="graw")
         gmx = keep.tile([P, 8], F32, name="gmx")
         gd = keep.tile([P, 8, E], F32, name="gd")
@@ -82,27 +87,38 @@ def tile_dcnv2lowrankexpertcross_x1_kernel(tc, x0, x, v, c, u, bias, gate, out, 
                 in_=u[e, :, dh * 512 : (dh + 1) * 512].rearrange("(p j) w -> p j w", j=4),
             )
 
-        nc.gpsimd.memset(warm[:], 0.0)
-        make_identity(nc, idf[:])
+        nc.vector.memset(pad[:], 0.0)
+        nc.vector.memset(bpad[:], 0.0)
+        nc.vector.memset(warm[:], 0.0)
+        nc.vector.memset(ones[:], 1.0)
         make_identity(nc, idb[:])
-        nc.gpsimd.memset(ones[:], 1.0)
-        nc.gpsimd.memset(bpad[:], 0.0)
-        nc.scalar.activation(out=warm[:], in_=warm[:], func=ACT.Tanh)
-
-        def load_v0(q):
-            cols = slice(256 * q, 256 * (q + 1))
-            nc.sync.dma_start(
-                out=vraw[0, 0][:, :, cols], in_=v[0, :512, cols].rearrange("(p j) w -> p j w", j=4)
-            )
+        make_identity(nc, idf[:])
 
         def load_bias():
-            nc.sync.dma_start(out=bpad[0:1, :], in_=bias.unsqueeze(0))
+            nc.scalar.dma_start(out=bpad[0:1, :], in_=bias.unsqueeze(0))
+
+        def warm_up():
+            nc.scalar.activation(out=warm[:], in_=warm[:], func=ACT.Tanh)
 
         def load_c():
-            nc.sync.dma_start(out=csb[:], in_=c.rearrange("e (p t) -> p e t", t=4))
+            nc.scalar.dma_start(out=pad[0:E, 0:512], in_=c)
 
         def load_gate():
-            nc.sync.dma_start(out=graw[:], in_=gate.rearrange("(i p) e -> p i e", p=P))
+            nc.scalar.dma_start(out=pad[0:8, 512:768], in_=gate.rearrange("(i p) e -> i (p e)", p=P))
+
+        small = {}
+
+        def small_turn():
+            small[0] = bank("aux", TB["aux"], BF16, name="sm")
+            for t in range(4):
+                nc.tensor.transpose(small[0][:, t * P : (t + 1) * P], pad[:, t:512:4], idb[:])
+            for e in range(E):
+                nc.tensor.transpose(small[0][:, (4 + e) * P : (5 + e) * P], pad[:, 512 + e : 768 : 2], idb[:])
+
+        def small_evac():
+            sm = small[0][:].rearrange("p (s r) -> p s r", r=P)
+            nc.scalar.copy(out=csb[:].rearrange("p e t -> p t e"), in_=sm[:, 0:4, 0:E])
+            nc.scalar.copy(out=graw[:].rearrange("p i e -> p e i"), in_=sm[:, 4:6, 0:8])
 
         xtr = {}
 
@@ -293,18 +309,37 @@ def tile_dcnv2lowrankexpertcross_x1_kernel(tc, x0, x, v, c, u, bias, gate, out, 
 
         otr = {}
 
+        cb = {}
+
+        def out_cast(k, a):
+            if a == 0:
+                cb[k] = work.tile([P, 2, 256], F32, name="cb", tag="cb", bufs=3)
+            nc.scalar.copy(
+                out=cb[k][:, a, :].bitcast(BF16).rearrange("p (u m w) -> p u m w", u=2, w=2),
+                in_=ot[k][:, a, :].rearrange("p (m u w) -> p u m w", u=2, w=2),
+            )
+
         def out_turn(k, a):
-            if True:
-                tr = bank("tr", TB["tr"])
-                for t in range(4):
-                    nc.tensor.transpose(tr[:, t * P : (t + 1) * P], ot[k][:, a, t::4], idf[:])
-                otr[k, a] = tr
+            if a == 0:
+                otr[k] = bank("tr", TB["tr"])
+            for w in range(2):
+                nc.tensor.transpose(
+                    otr[k][:, (2 * a + w) * P : (2 * a + w + 1) * P], cb[k][:, a, w * P : (w + 1) * P], idf[:]
+                )
 
         def out_evac(k, a):
-            if a == 0:
-                qb[k] = work.tile([P, 256, 4], BF16, name="qb", tag="qb", bufs=3, align_bytes=64)
-            if True:
-                nc.scalar.copy(out=qb[k][:, a * P : (a + 1) * P, :], in_=otr[k, a][:].rearrange("p (t r) -> p r t", t=4))
+            if a != 1:
+                qb[k] = work.tile([P, 256, 2], F32, name="qb", tag="qb", bufs=3, align_bytes=64)
+            if a == 2:
+                nc.scalar.copy(
+                    out=qb[k][:].rearrange("p (a r) u -> p a r u", a=2),
+                    in_=otr[k][:].rearrange("p (a u r) -> p a r u", a=2, u=2),
+                )
+            else:
+                nc.scalar.copy(
+                    out=qb[k][:, a * P : (a + 1) * P, :],
+                    in_=otr[k][:, 256 * a : 256 * (a + 1)].rearrange("p (u r) -> p r u", u=2),
+                )
 
         wqs = {}
 
@@ -319,7 +354,7 @@ def tile_dcnv2lowrankexpertcross_x1_kernel(tc, x0, x, v, c, u, bias, gate, out, 
                 r0 = i0 * P + n * a
                 nc.vector.quantize_mx(
                     out=wq[:, n * a : n * (a + 1)].bitcast(FP8X4), scales=osc[r0 // 512][:, dh, r0 % 512 : r0 % 512 + n],
-                    in_=qb[k][:, n * a : n * (a + 1), :].rearrange("p b t -> p (b t)"),
+                    in_=qb[k][:, n * a : n * (a + 1), :].rearrange("p b u -> p (b u)").bitcast(BF16),
                 )
                 nc.sync.dma_start(
                     out=words[dh, :, r0 : r0 + n, :].rearrange("p m t -> p (m t)").bitcast(I32),
@@ -375,293 +410,304 @@ def tile_dcnv2lowrankexpertcross_x1_kernel(tc, x0, x, v, c, u, bias, gate, out, 
                 op=ALU.mult,
             )
 
-        load_v0(0)
-        load_gate()
-        load_v(0, 1)
+        load_v(0, 0)
         load_x(xs, x, 0)
-        x_turn(0)
         load_x(xs, x, 1)
+        load_v(0, 1)
+        load_c()
+        load_gate()
         load_bias()
-        x_evac(0)
-        bias_mm(0)
-        gate1()
-        v_inter(0, 0, 0)
-        bias_mm(1)
-        x_turn(1)
-        v_inter(0, 1, 0)
-        load_v0(1)
+        warm_up()
         load_v(1, 0)
-        v_move(1, 0, 0)
-        load_v(1, 1)
-        bias_evac(0)
-        gate2()
+        x_turn(0)
+        x_turn(1)
+        x_evac(0)
+        v_inter(0, 0, 0)
+        small_turn()
+        v_inter(0, 0, 1)
         x_evac(1)
-        gate3()
-        load_u(0, 0)
-        v_inter(0, 1, 1)
+        v_quant(0, 0)
+        load_v(1, 1)
+        small_evac()
+        bias_mm(0)
+        bias_evac(0)
+        bias_mm(1)
         bias_evac(1)
-        gate4()
-        v_evac(1, 0, 0)
+        v_move(1, 0, 0)
+        v_inter(0, 1, 0)
+        x_quant(0)
+        gate1()
+        gate2()
+        load_u(0, 0)
+        load_u(1, 0)
         v_move(1, 0, 1)
+        gate3()
+        v_evac(1, 0, 0)
+        v_inter(0, 1, 1)
+        gate4()
+        v_move(1, 1, 0)
+        v_move(1, 1, 1)
         v_quant(0, 1)
         v_evac(1, 0, 1)
-        v_move(1, 1, 0)
-        load_u(1, 0)
-        v_move(1, 1, 1)
-        v_evac(1, 1, 0)
-        u_move(0, 0, 0)
-        v_inter(0, 0, 1)
-        load_c()
-        v_evac(1, 1, 1)
         load_x(xs, x, 2)
-        v_quant(0, 0)
-        load_x(xs, x, 3)
-        x_quant(0)
         stage1(0, 0, 0)
         stage1(0, 0, 1)
+        u_move(0, 0, 0)
         gate5()
-        v_quant(1, 0)
-        u_evac(0, 0, 0)
+        v_evac(1, 1, 0)
+        v_evac(1, 1, 1)
         tanh(0, 0, 0)
         tanh(0, 0, 1)
-        v_quant(1, 1)
-        u_move(0, 0, 1)
-        load_x(x0s, x0, 0)
-        stage1(1, 0, 0)
-        stage1(1, 0, 1)
+        u_evac(0, 0, 0)
+        load_x(xs, x, 3)
         u_move(1, 0, 0)
-        load_x(xs, x, 4)
-        h_mult(0, 0)
-        u_evac(0, 0, 1)
-        u_quant(0, 0)
-        h_quant(0, 0)
-        load_u(1, 1)
-        load_x(x0s, x0, 2)
-        u_move(1, 0, 1)
         gate6()
-        tanh(1, 0, 0)
-        tanh(1, 0, 1)
-        x_turn(2)
+        v_quant(1, 0)
+        load_x(x0s, x0, 0)
         u_evac(1, 0, 0)
-        x_turn(3)
-        h_mult(1, 0)
-        y_mm(0, 0)
-        load_u(0, 1)
-        u_evac(1, 0, 1)
-        load_x(xs, x, 6)
-        x_evac(2)
         load_x(x0s, x0, 1)
-        x_turn(4)
-        u_quant(1, 0)
+        v_quant(1, 1)
+        x_turn(2)
+        h_mult(0, 0)
+        x_turn(3)
+        load_u(0, 1)
+        load_u(1, 1)
+        stage1(1, 0, 0)
+        x_evac(2)
+        load_x(x0s, x0, 2)
+        load_x(x0s, x0, 3)
         x_evac(3)
-        h_quant(1, 0)
-        mix0(0, 0)
-        resid_v(3, 1)
-        y_mm(0, 1)
-        mix0(0, 1)
-        load_x(xs, x, 5)
-        u_inter(0, 1, 0)
-        x_evac(4)
+        u_move(0, 0, 1)
+        tanh(1, 0, 0)
+        stage1(1, 0, 1)
+        u_evac(0, 0, 1)
+        tanh(1, 0, 1)
+        load_x(xs, x, 4)
+        h_quant(0, 0)
+        u_move(1, 0, 1)
         x_quant(1)
-        u_inter(0, 1, 1)
-        x_turn(5)
+        u_quant(0, 0)
+        h_mult(1, 0)
+        u_evac(1, 0, 1)
         stage1(0, 1, 0)
         tanh(0, 1, 0)
+        load_x(xs, x, 5)
+        u_quant(1, 0)
         stage1(0, 1, 1)
+        cf_copy()
         tanh(0, 1, 1)
-        x_turn(6)
-        load_x(xs, x, 7)
-        x_evac(5)
-        mix1(0, 0)
+        y_mm(0, 0)
+        h_quant(1, 0)
+        mix0(0, 0)
+        y_mm(0, 1)
         stage1(1, 1, 0)
+        h_mult(0, 1)
+        u_inter(0, 1, 0)
+        mix0(0, 1)
+        x_turn(4)
+        x_turn(5)
+        load_x(xs, x, 6)
+        h_quant(0, 1)
+        mix1(0, 0)
+        stage1(1, 1, 1)
+        u_inter(1, 1, 0)
+        y_mm(1, 0)
+        load_x(xs, x, 7)
         mix1(0, 1)
         tanh(1, 1, 0)
+        x_evac(4)
         cross(0, 0)
-        cross(0, 1)
-        stage1(1, 1, 1)
-        resid_v(0, 0)
-        u_quant(0, 1)
-        tanh(1, 1, 1)
         x_turn(7)
-        h_mult(0, 1)
+        cross(0, 1)
+        x_evac(5)
+        tanh(1, 1, 1)
+        resid_v(0, 0)
         x_quant(2)
-        load_x(x0s, x0, 5)
-        u_inter(1, 1, 0)
-        h_quant(0, 1)
-        x_evac(6)
+        u_inter(1, 1, 1)
         h_mult(1, 1)
-        cf_copy()
-        stage1(1, 2, 0)
-        y_mm(1, 0)
-        resid_v(2, 1)
         mix0(1, 0)
-        load_x(x0s, x0, 3)
+        x_turn(6)
+        u_inter(0, 1, 1)
         h_quant(1, 1)
-        stage1(0, 2, 0)
-        tanh(0, 2, 0)
-        resid_g(0, 1)
-        y_mm(3, 0)
         mix0(1, 1)
-        mix0(3, 0)
+        u_quant(1, 1)
+        stage1(1, 2, 0)
+        x_evac(6)
         y_mm(1, 1)
         mix1(1, 0)
-        mix0(3, 1)
-        mix1(1, 1)
-        tanh(1, 2, 0)
-        resid_g(0, 0)
-        u_inter(1, 1, 1)
-        stage1(1, 2, 1)
-        load_x(x0s, x0, 6)
+        stage1(0, 2, 0)
         x_evac(7)
-        tanh(1, 2, 1)
-        cross(1, 0)
+        u_quant(0, 1)
+        tanh(1, 2, 0)
+        resid_g(0, 1)
+        resid_v(4, 1)
+        resid_g(0, 0)
+        out_cast(0, 0)
+        stage1(1, 2, 1)
+        y_mm(3, 0)
+        mix1(1, 1)
         load_x(x0s, x0, 4)
-        out_turn(0, 0)
-        h_scale(1, 2)
-        u_quant(1, 1)
-        stage1(0, 2, 1)
-        resid_v(0, 1)
+        y_mm(3, 1)
+        cross(1, 0)
+        resid_v(2, 1)
         x_quant(3)
-        y_mm(2, 0)
-        mix0(2, 0)
+        tanh(1, 2, 1)
+        resid_v(1, 1)
+        tanh(0, 2, 0)
+        stage1(1, 3, 0)
+        mix0(3, 0)
+        resid_v(3, 1)
+        resid_v(1, 0)
+        out_turn(0, 0)
+        mix0(3, 1)
         cross(1, 1)
-        h_move(1, 2)
+        mix1(3, 0)
+        load_x(x0s, x0, 5)
+        mix1(3, 1)
+        h_scale(1, 2)
+        tanh(1, 3, 0)
+        resid_g(1, 0)
+        out_cast(0, 1)
+        cross(3, 0)
+        stage1(0, 2, 1)
+        cross(3, 1)
+        stage1(1, 3, 1)
+        y_mm(2, 0)
         tanh(0, 2, 1)
+        h_move(1, 2)
+        y_mm(2, 1)
+        resid_v(3, 0)
+        store_out(0)
+        out_turn(0, 1)
+        resid_g(1, 1)
+        h_mult(0, 2)
+        mix0(2, 0)
+        tanh(1, 3, 1)
+        out_cast(1, 0)
+        load_x(x0s, x0, 6)
+        h_scale(1, 3)
+        h_quant(0, 2)
+        store_out(1)
+        resid_g(3, 1)
+        stage1(0, 3, 0)
         mix0(2, 1)
         h_evac(1, 2)
-        y_mm(2, 1)
-        out_turn(0, 1)
-        stage1(0, 3, 0)
-        resid_v(1, 0)
-        store_out(0)
-        out_evac(0, 0)
         mix1(2, 0)
-        mix1(2, 1)
-        out_evac(0, 1)
-        h_quant(1, 2)
-        resid_v(4, 1)
-        y_mm(3, 1)
-        cross(2, 0)
-        resid_g(1, 0)
-        resid_g(1, 1)
-        mix1(3, 0)
-        h_mult(0, 2)
-        resid_v(2, 0)
-        out_turn(1, 0)
-        stage1(1, 3, 0)
-        out_turn(1, 1)
-        tanh(0, 3, 0)
-        tanh(1, 3, 0)
-        stage1(1, 3, 1)
-        out_evac(1, 0)
-        cross(3, 0)
-        resid_v(6, 1)
-        h_quant(0, 2)
-        resid_v(5, 1)
         y_mm(4, 0)
-        mix1(3, 1)
-        out_quant(0)
-        mix0(4, 0)
-        resid_v(3, 0)
-        y_mm(5, 0)
-        cross(2, 1)
+        h_quant(1, 2)
+        tanh(0, 3, 0)
         resid_g(3, 0)
+        mix0(4, 0)
         stage1(0, 3, 1)
-        out_evac(1, 1)
-        tanh(1, 3, 1)
+        mix1(2, 1)
         mix0(4, 1)
-        h_scale(1, 3)
-        tanh(0, 3, 1)
-        resid_g(2, 0)
-        h_scale(0, 3)
-        store_out(1)
-        out_quant(1)
-        cross(3, 1)
         y_mm(4, 1)
-        h_move(1, 3)
-        h_evac(1, 3)
-        resid_g(2, 1)
-        mix1(4, 0)
-        h_move(0, 3)
-        mix0(5, 0)
-        resid_g(3, 1)
-        h_evac(0, 3)
-        mix0(5, 1)
-        h_quant(1, 3)
-        mix1(4, 1)
         y_mm(5, 1)
-        h_quant(0, 3)
-        out_turn(3, 0)
+        mix1(4, 0)
+        out_evac(0, 2)
+        mix1(4, 1)
+        out_cast(3, 0)
+        h_move(1, 3)
+        tanh(0, 3, 1)
+        h_scale(0, 3)
+        out_quant(0)
+        out_cast(3, 1)
+        y_mm(5, 0)
+        out_cast(1, 1)
+        out_turn(1, 0)
+        cross(2, 0)
+        h_move(0, 3)
+        h_evac(1, 3)
+        cross(2, 1)
+        mix0(5, 0)
+        resid_v(2, 0)
+        h_evac(0, 3)
+        out_turn(1, 1)
+        out_evac(1, 2)
         cross(4, 0)
-        store_out(2)
-        store_out(3)
-        out_evac(3, 0)
-        out_turn(2, 0)
-        out_turn(3, 1)
-        mix1(5, 0)
-        y_mm(6, 0)
-        out_evac(2, 0)
-        out_evac(3, 1)
+        h_quant(1, 3)
+        resid_g(2, 1)
+        mix0(5, 1)
         resid_v(4, 0)
-        out_turn(2, 1)
-        mix1(5, 1)
+        out_turn(3, 0)
+        out_turn(3, 1)
+        load_x(x0s, x0, 7)
+        h_quant(0, 3)
+        out_evac(3, 2)
+        store_out(3)
+        mix1(5, 0)
         cross(4, 1)
-        out_evac(2, 1)
-        resid_g(4, 0)
+        resid_v(5, 1)
+        out_quant(1)
+        resid_g(2, 0)
+        out_cast(2, 0)
+        mix1(5, 1)
+        out_quant(3)
+        out_turn(2, 0)
+        y_mm(6, 0)
         cross(5, 0)
         mix0(6, 0)
-        load_x(x0s, x0, 7)
-        out_quant(3)
+        resid_v(0, 1)
+        cross(5, 1)
+        resid_g(4, 0)
+        out_cast(2, 1)
+        out_cast(4, 0)
+        out_turn(4, 0)
+        store_out(2)
+        resid_g(4, 1)
         resid_v(5, 0)
         y_mm(6, 1)
-        out_quant(2)
-        mix1(6, 0)
-        mix0(6, 1)
-        cross(5, 1)
-        mix1(6, 1)
-        resid_g(4, 1)
-        cross(6, 0)
-        y_mm(7, 0)
-        store_out(4)
-        cross(6, 1)
-        mix0(7, 0)
-        y_mm(7, 1)
-        out_turn(4, 0)
         resid_g(5, 0)
-        store_scales(0)
-        resid_v(6, 0)
-        out_turn(4, 1)
-        out_evac(4, 0)
-        mix1(7, 0)
-        mix0(7, 1)
-        out_turn(5, 0)
+        out_cast(4, 1)
         resid_g(5, 1)
-        out_evac(4, 1)
-        cross(7, 0)
-        mix1(7, 1)
-        out_evac(5, 0)
+        out_cast(5, 0)
+        out_turn(4, 1)
+        mix0(6, 1)
+        store_out(4)
+        mix1(6, 0)
+        out_turn(2, 1)
+        out_evac(2, 2)
+        mix1(6, 1)
+        out_evac(4, 2)
+        y_mm(7, 1)
+        cross(6, 0)
         store_out(5)
-        out_turn(5, 1)
-        out_evac(5, 1)
-        resid_v(7, 0)
-        resid_g(6, 1)
-        resid_g(6, 0)
-        out_turn(6, 0)
-        store_out(6)
-        out_evac(6, 0)
+        cross(6, 1)
         out_quant(4)
+        resid_v(6, 0)
+        resid_v(6, 1)
+        resid_g(6, 0)
+        y_mm(7, 0)
+        mix0(7, 0)
+        mix0(7, 1)
+        out_quant(2)
+        resid_g(6, 1)
+        mix1(7, 0)
+        mix1(7, 1)
+        cross(7, 0)
+        out_cast(5, 1)
+        out_cast(6, 0)
+        out_turn(5, 0)
+        out_turn(5, 1)
+        out_evac(5, 2)
+        store_out(6)
+        out_turn(6, 0)
+        out_cast(6, 1)
         cross(7, 1)
-        store_out(7, (0,))
-        out_quant(5)
-        out_turn(7, 0)
-        resid_v(1, 1)
-        out_evac(7, 0)
         out_turn(6, 1)
+        resid_v(7, 0)
+        store_scales(0)
         resid_v(7, 1)
-        store_out(7, (1,))
-        out_turn(7, 1)
-        out_evac(6, 1)
+        out_evac(6, 2)
+        out_cast(7, 0)
+        out_cast(7, 1)
+        store_out(7, (0,))
+        out_turn(7, 0)
         out_quant(6)
+        out_quant(5)
+        store_out(7, (1,))
+        out_evac(7, 0)
+        out_turn(7, 1)
         out_quant(7)
         out_evac(7, 1)
         out_quant(7, 1)

@@ -17,8 +17,6 @@ ACT = mybir.ActivationFunctionType
 P = 128
 
 YB, AUXB, TRB = 4, 2, 2
-GSP = {k: (256, 512) for k in range(7)}
-GSP[7] = (0, 0)
 
 
 def tile_dcnv2lowrankexpertcross_x1_kernel(tc, x0, x, v, c, u, bias, gate, out, words, scales):
@@ -50,8 +48,8 @@ def tile_dcnv2lowrankexpertcross_x1_kernel(tc, x0, x, v, c, u, bias, gate, out, 
         xg = [keep.tile([P, 2, 256, 2], F32, name=f"xg{h}", align_bytes=64) for h in range(4)]
         xc = [keep.tile([P, 2, 256], U32, name=f"xc{h}", align_bytes=64) for h in range(4)]
         xsc = [keep.tile([P, 2, 256], U8, name=f"xsc{h}", align_bytes=64) for h in range(4)]
-        hc = {(e, h): keep.tile([P, 256], U32, name=f"hc{e}{h}", align_bytes=64) for e in range(E) for h in range(4)}
-        hs = {(e, h): keep.tile([P, 256], U8, name=f"hs{e}{h}", align_bytes=64) for e in range(E) for h in range(4)}
+        hc = [keep.tile([P, E, 256], U32, name=f"hc{h}", align_bytes=64) for h in range(4)]
+        hs = [keep.tile([P, E, 256], U8, name=f"hs{h}", align_bytes=64) for h in range(4)]
         osc = [keep.tile([P, 2, 512], U8, name=f"osc{h}", align_bytes=64) for h in range(2)]
         cf = keep.tile([P, E, 4], F32, name="cf")
         csb = keep.tile([P, E, 4], BF16, name="csb")
@@ -157,9 +155,10 @@ def tile_dcnv2lowrankexpertcross_x1_kernel(tc, x0, x, v, c, u, bias, gate, out, 
         def vdst(e, g, q):
             return vg[e, g][:].rearrange("p (t m j) -> p t m j", t=4, j=4)[:, :, 64 * q : 64 * (q + 1), :]
 
-        def v_inter(e, g, q):
+        def v_inter(e, g):
             nc.vector.tensor_copy(
-                out=vdst(e, g, q), in_=vraw[e, g][:, :, 256 * q : 256 * (q + 1)].rearrange("p j (m t) -> p t m j", t=4)
+                out=vg[e, g][:].rearrange("p (t m j) -> p t m j", t=4, j=4),
+                in_=vraw[e, g][:].rearrange("p j (m t) -> p t m j", t=4),
             )
 
         def v_move(e, g, q, tag="y"):
@@ -204,39 +203,49 @@ def tile_dcnv2lowrankexpertcross_x1_kernel(tc, x0, x, v, c, u, bias, gate, out, 
                     )
 
         def tanh(e, h, q):
-            if q == 0:
-                th[e, h] = work.tile([P, 4, 256], F32, name="th", tag="th", bufs=4)
+            if e == 0 and q == 0:
+                th[h] = work.tile([P, E, 4, 256], F32, name="th", tag="th", bufs=2)
             nc.scalar.activation(
-                out=th[e, h][:, 2 * q : 2 * q + 2, :].rearrange("p t b -> p (t b)"), in_=acc1[e, h, q][:], func=ACT.Tanh
+                out=th[h][:, e, 2 * q : 2 * q + 2, :].rearrange("p t b -> p (t b)"), in_=acc1[e, h, q][:], func=ACT.Tanh
             )
 
-        def new_hb(e, h):
-            hb[e, h] = work.tile([P, 256, 4], BF16, name="hb", tag="hb", bufs=3, align_bytes=64)
+        def new_hb(h):
+            hb[h] = work.tile([P, E, 256, 4], BF16, name="hb", tag="hb", bufs=2, align_bytes=64)
 
-        def h_mult(e, h):
-            new_hb(e, h)
+        def h_mult(h, e0, n):
+            if e0 == 0:
+                new_hb(h)
             nc.vector.tensor_tensor(
-                out=hb[e, h][:],
-                in0=th[e, h][:].rearrange("p t b -> p b t"),
-                in1=csb[:, e, :].unsqueeze(1).to_broadcast([P, 256, 4]),
+                out=hb[h][:, e0 : e0 + n, :, :],
+                in0=th[h][:, e0 : e0 + n, :, :].rearrange("p e t b -> p e b t"),
+                in1=csb[:, e0 : e0 + n, :].unsqueeze(2).to_broadcast([P, n, 256, 4]),
                 op=ALU.mult,
             )
 
-        def h_scale(e, h):
-            ht[e, h] = work.tile([P, 4, 256], BF16, name="ht", tag="ht")
+        def h_scale(h, e):
+            if e == 0:
+                ht[h] = work.tile([P, E, 4, 256], BF16, name="ht", tag="ht", bufs=1)
             for t in range(4):
-                nc.scalar.activation(out=ht[e, h][:, t, :], in_=th[e, h][:, t, :], func=ACT.Copy, scale=cf[:, e, t : t + 1])
+                nc.scalar.activation(out=ht[h][:, e, t, :], in_=th[h][:, e, t, :], func=ACT.Copy, scale=cf[:, e, t : t + 1])
 
-        def h_move(e, h):
-            move("aux", ("h", e, h), ht[e, h])
+        def h_inter(h, e):
+            if e == 0:
+                new_hb(h)
+            nc.scalar.copy(out=hb[h][:, e, :, :], in_=ht[h][:, e, :, :].rearrange("p t b -> p b t"))
 
-        def h_evac(e, h):
-            new_hb(e, h)
-            nc.scalar.copy(out=hb[e, h][:], in_=mvs["h", e, h].rearrange("p t b -> p b t"))
+        def h_move(h, e):
+            move("aux", ("h", e, h), ht[h][:, e, :, :])
 
-        def h_quant(e, h):
+        def h_evac(h, e):
+            if e == 0:
+                new_hb(h)
+            nc.scalar.copy(out=hb[h][:, e, :, :], in_=mvs["h", e, h].rearrange("p t b -> p b t"))
+
+        def h_quant(h, e0, n):
             nc.vector.quantize_mx(
-                out=hc[e, h][:].bitcast(FP8X4), scales=hs[e, h][:], in_=hb[e, h][:].rearrange("p b t -> p (b t)")
+                out=hc[h][:, e0 : e0 + n, :].rearrange("p e b -> p (e b)").bitcast(FP8X4),
+                scales=hs[h][:, e0 : e0 + n, :].rearrange("p e b -> p (e b)"),
+                in_=hb[h][:, e0 : e0 + n, :, :].rearrange("p e b t -> p (e b t)"),
             )
 
         pairs = [(0, 0), (2, 0), (0, 1), (2, 1), (4, 0), (4, 1), (6, 0), (6, 1)]
@@ -252,8 +261,8 @@ def tile_dcnv2lowrankexpertcross_x1_kernel(tc, x0, x, v, c, u, bias, gate, out, 
                     ys[k, e, a] = bank("y", TB["y"], name="y")
                     nc.tensor.matmul_mx(
                         out=ys[k, e, a][:],
-                        lhsT=hc[e, h][:, li * P : (li + 1) * P].bitcast(FP8X4),
-                        lhsT_scale=hs[e, h][:, li * P : (li + 1) * P],
+                        lhsT=hc[h][:, e, li * P : (li + 1) * P].bitcast(FP8X4),
+                        lhsT_scale=hs[h][:, e, li * P : (li + 1) * P],
                         rhs=uc[e, dh][:].bitcast(FP8X4),
                         rhs_scale=us[e, dh][:],
                         start=True,
@@ -276,28 +285,26 @@ def tile_dcnv2lowrankexpertcross_x1_kernel(tc, x0, x, v, c, u, bias, gate, out, 
                 in1=sa[k][0][:, a, :], op0=ALU.mult, op1=ALU.add,
             )
 
-        def cross(k, a):
+        def mix(k):
+            for a in range(2):
+                mix0(k, a)
+            for a in range(2):
+                mix1(k, a)
+
+        def cross(k, a0, n):
             i0, dh = pairs[k]
             cols = slice(dh * 512, (dh + 1) * 512)
-            nc.vector.tensor_tensor(out=sa[k][2][:, a, :], in0=sa[k][1][:, a, :], in1=x0s[:, i0 + a, cols], op=ALU.mult)
-            if a == 0:
+            nc.vector.tensor_tensor(
+                out=sa[k][2][:, a0 : a0 + n, :], in0=sa[k][1][:, a0 : a0 + n, :], in1=x0s[:, i0 + a0 : i0 + a0 + n, cols], op=ALU.mult
+            )
+            if a0 == 0:
                 ot[k] = work.tile([P, 2, 512], F32, name="ot", tag="ot", bufs=3)
 
-        def add_x(eng, k, a, lo, hi):
+        def resid(eng, k, a):
             i0, dh = pairs[k]
             eng.tensor_tensor(
-                out=ot[k][:, a, lo:hi], in0=sa[k][2][:, a, lo:hi], in1=xs[:, i0 + a, dh * 512 + lo : dh * 512 + hi], op=ALU.add
+                out=ot[k][:, a, :], in0=sa[k][2][:, a, :], in1=xs[:, i0 + a, dh * 512 : (dh + 1) * 512], op=ALU.add
             )
-
-        def resid_v(k, a):
-            split = 512 - GSP[k][a]
-            if split > 0:
-                add_x(nc.vector, k, a, 0, split)
-
-        def resid_g(k, a):
-            split = 512 - GSP[k][a]
-            if split < 512:
-                add_x(nc.gpsimd, k, a, split, 512)
 
         def store_out(k, which=(0, 1)):
             i0, dh = pairs[k]
@@ -311,12 +318,12 @@ def tile_dcnv2lowrankexpertcross_x1_kernel(tc, x0, x, v, c, u, bias, gate, out, 
 
         cb = {}
 
-        def out_cast(k, a):
-            if a == 0:
-                cb[k] = work.tile([P, 2, 256], F32, name="cb", tag="cb", bufs=3)
+        def out_cast(k, a0, n):
+            if a0 == 0:
+                cb[k] = work.tile([P, 2, 256], F32, name="cb", tag="cb", bufs=2)
             nc.scalar.copy(
-                out=cb[k][:, a, :].bitcast(BF16).rearrange("p (u m w) -> p u m w", u=2, w=2),
-                in_=ot[k][:, a, :].rearrange("p (m u w) -> p u m w", u=2, w=2),
+                out=cb[k][:, :, P * a0 : P * (a0 + n)].bitcast(BF16).rearrange("p u (m w) -> p u m w", w=2),
+                in_=ot[k][:, a0 : a0 + n, :].rearrange("p a (m u w) -> p u (a m) w", u=2, w=2),
             )
 
         def out_turn(k, a):
@@ -324,7 +331,7 @@ def tile_dcnv2lowrankexpertcross_x1_kernel(tc, x0, x, v, c, u, bias, gate, out, 
                 otr[k] = bank("tr", TB["tr"])
             for w in range(2):
                 nc.tensor.transpose(
-                    otr[k][:, (2 * a + w) * P : (2 * a + w + 1) * P], cb[k][:, a, w * P : (w + 1) * P], idf[:]
+                    otr[k][:, (2 * a + w) * P : (2 * a + w + 1) * P], cb[k][:, w, a * P : (a + 1) * P], idf[:]
                 )
 
         def out_evac(k, a):
@@ -420,295 +427,229 @@ def tile_dcnv2lowrankexpertcross_x1_kernel(tc, x0, x, v, c, u, bias, gate, out, 
         warm_up()
         load_v(1, 0)
         x_turn(0)
-        x_turn(1)
-        x_evac(0)
-        v_inter(0, 0, 0)
-        small_turn()
-        v_inter(0, 0, 1)
-        x_evac(1)
+        v_inter(0, 0)
         v_quant(0, 0)
         load_v(1, 1)
-        small_evac()
-        bias_mm(0)
-        bias_evac(0)
-        bias_mm(1)
-        bias_evac(1)
-        v_move(1, 0, 0)
-        v_inter(0, 1, 0)
-        x_quant(0)
-        gate1()
-        gate2()
+        x_turn(1)
+        small_turn()
+        x_evac(0)
         load_u(0, 0)
+        v_inter(0, 1)
+        small_evac()
         load_u(1, 0)
-        v_move(1, 0, 1)
-        gate3()
-        v_evac(1, 0, 0)
-        v_inter(0, 1, 1)
-        gate4()
-        v_move(1, 1, 0)
-        v_move(1, 1, 1)
+        bias_mm(0)
+        gate1()
+        bias_mm(1)
+        x_evac(1)
         v_quant(0, 1)
-        v_evac(1, 0, 1)
-        load_x(xs, x, 2)
-        stage1(0, 0, 0)
-        stage1(0, 0, 1)
-        u_move(0, 0, 0)
-        gate5()
+        x_quant(0)
+        bias_evac(0)
+        gate2()
+        v_move(1, 1, 0)
+        bias_evac(1)
+        v_move(1, 1, 1)
+        gate3()
         v_evac(1, 1, 0)
+        stage1(0, 0, 0)
         v_evac(1, 1, 1)
-        tanh(0, 0, 0)
-        tanh(0, 0, 1)
-        u_evac(0, 0, 0)
+        u_move(0, 0, 0)
+        stage1(0, 0, 1)
+        u_move(0, 0, 1)
+        gate4()
+        load_x(xs, x, 2)
+        v_inter(1, 0)
+        gate5()
         load_x(xs, x, 3)
-        u_move(1, 0, 0)
-        gate6()
         v_quant(1, 0)
-        load_x(x0s, x0, 0)
-        u_evac(1, 0, 0)
-        load_x(x0s, x0, 1)
         v_quant(1, 1)
+        load_x(x0s, x0, 0)
         x_turn(2)
-        h_mult(0, 0)
-        x_turn(3)
+        tanh(0, 0, 0)
+        u_evac(0, 0, 0)
+        gate6()
+        load_x(x0s, x0, 1)
         load_u(0, 1)
         load_u(1, 1)
+        x_turn(3)
+        tanh(0, 0, 1)
+        u_evac(0, 0, 1)
+        h_mult(0, 0, 1)
+        stage1(1, 0, 1)
         stage1(1, 0, 0)
         x_evac(2)
+        u_move(1, 0, 0)
         load_x(x0s, x0, 2)
         load_x(x0s, x0, 3)
         x_evac(3)
-        u_move(0, 0, 1)
-        tanh(1, 0, 0)
-        stage1(1, 0, 1)
-        u_evac(0, 0, 1)
         tanh(1, 0, 1)
-        load_x(xs, x, 4)
-        h_quant(0, 0)
         u_move(1, 0, 1)
-        x_quant(1)
+        tanh(1, 0, 0)
         u_quant(0, 0)
-        h_mult(1, 0)
-        u_evac(1, 0, 1)
+        x_quant(1)
+        u_evac(1, 0, 0)
+        h_quant(0, 0, 1)
         stage1(0, 1, 0)
+        h_mult(0, 1, 1)
+        stage1(1, 1, 1)
+        load_x(xs, x, 4)
+        u_evac(1, 0, 1)
         tanh(0, 1, 0)
-        load_x(xs, x, 5)
         u_quant(1, 0)
+        h_quant(0, 1, 1)
+        load_x(xs, x, 5)
+        y_mm(0, 0)
+        load_x(xs, x, 6)
+        tanh(1, 1, 1)
+        load_x(xs, x, 7)
         stage1(0, 1, 1)
         cf_copy()
         tanh(0, 1, 1)
-        y_mm(0, 0)
-        h_quant(1, 0)
-        mix0(0, 0)
-        y_mm(0, 1)
         stage1(1, 1, 0)
-        h_mult(0, 1)
-        u_inter(0, 1, 0)
-        mix0(0, 1)
+        y_mm(0, 1)
         x_turn(4)
         x_turn(5)
-        load_x(xs, x, 6)
-        h_quant(0, 1)
-        mix1(0, 0)
-        stage1(1, 1, 1)
-        u_inter(1, 1, 0)
-        y_mm(1, 0)
-        load_x(xs, x, 7)
-        mix1(0, 1)
+        mix(0)
         tanh(1, 1, 0)
+        u_inter(0, 1, 0)
+        h_mult(1, 0, 2)
         x_evac(4)
-        cross(0, 0)
         x_turn(7)
-        cross(0, 1)
         x_evac(5)
-        tanh(1, 1, 1)
-        resid_v(0, 0)
-        x_quant(2)
-        u_inter(1, 1, 1)
-        h_mult(1, 1)
-        mix0(1, 0)
-        x_turn(6)
         u_inter(0, 1, 1)
-        h_quant(1, 1)
-        mix0(1, 1)
-        u_quant(1, 1)
-        stage1(1, 2, 0)
-        x_evac(6)
-        y_mm(1, 1)
-        mix1(1, 0)
+        x_quant(2)
+        h_quant(1, 0, 2)
+        x_turn(6)
         stage1(0, 2, 0)
-        x_evac(7)
         u_quant(0, 1)
-        tanh(1, 2, 0)
-        resid_g(0, 1)
-        resid_v(4, 1)
-        resid_g(0, 0)
-        out_cast(0, 0)
-        stage1(1, 2, 1)
-        y_mm(3, 0)
-        mix1(1, 1)
-        load_x(x0s, x0, 4)
-        y_mm(3, 1)
-        cross(1, 0)
-        resid_v(2, 1)
-        x_quant(3)
-        tanh(1, 2, 1)
-        resid_v(1, 1)
+        y_mm(1, 0)
+        y_mm(1, 1)
+        u_inter(1, 1, 0)
+        x_evac(6)
         tanh(0, 2, 0)
-        stage1(1, 3, 0)
-        mix0(3, 0)
-        resid_v(3, 1)
-        resid_v(1, 0)
-        out_turn(0, 0)
-        mix0(3, 1)
-        cross(1, 1)
-        mix1(3, 0)
-        load_x(x0s, x0, 5)
-        mix1(3, 1)
-        h_scale(1, 2)
-        tanh(1, 3, 0)
-        resid_g(1, 0)
-        out_cast(0, 1)
-        cross(3, 0)
+        u_inter(1, 1, 1)
+        cross(0, 0, 2); mix(1)
+        u_quant(1, 1)
+        x_evac(7)
         stage1(0, 2, 1)
-        cross(3, 1)
-        stage1(1, 3, 1)
-        y_mm(2, 0)
         tanh(0, 2, 1)
-        h_move(1, 2)
+        resid(nc.gpsimd, 0, 1)
+        stage1(1, 2, 1)
+        resid(nc.vector, 0, 0)
+        y_mm(2, 0)
+        load_x(x0s, x0, 4)
+        tanh(1, 2, 1)
+        stage1(1, 2, 0)
+        x_quant(3)
         y_mm(2, 1)
-        resid_v(3, 0)
-        store_out(0)
-        out_turn(0, 1)
-        resid_g(1, 1)
-        h_mult(0, 2)
-        mix0(2, 0)
-        tanh(1, 3, 1)
-        out_cast(1, 0)
-        load_x(x0s, x0, 6)
-        h_scale(1, 3)
-        h_quant(0, 2)
-        store_out(1)
-        resid_g(3, 1)
+        h_scale(2, 0)
+        cross(1, 0, 2); mix(2)
+        resid(nc.gpsimd, 1, 1)
         stage1(0, 3, 0)
-        mix0(2, 1)
-        h_evac(1, 2)
-        mix1(2, 0)
-        y_mm(4, 0)
-        h_quant(1, 2)
+        tanh(1, 2, 0)
+        h_scale(2, 1)
+        resid(nc.vector, 1, 0)
+        h_move(2, 0)
+        y_mm(3, 0)
+        store_out(1)
+        y_mm(3, 1)
+        cross(2, 0, 2); mix(3)
         tanh(0, 3, 0)
-        resid_g(3, 0)
-        mix0(4, 0)
+        out_cast(0, 0, 2)
+        h_move(2, 1)
+        out_turn(0, 0)
+        h_evac(2, 0)
+        h_evac(2, 1)
+        h_quant(2, 0, 2)
         stage1(0, 3, 1)
-        mix1(2, 1)
-        mix0(4, 1)
-        y_mm(4, 1)
-        y_mm(5, 1)
-        mix1(4, 0)
-        out_evac(0, 2)
-        mix1(4, 1)
-        out_cast(3, 0)
-        h_move(1, 3)
-        tanh(0, 3, 1)
-        h_scale(0, 3)
-        out_quant(0)
-        out_cast(3, 1)
-        y_mm(5, 0)
-        out_cast(1, 1)
+        stage1(1, 3, 0)
+        out_cast(1, 0, 2)
+        resid(nc.gpsimd, 2, 1)
         out_turn(1, 0)
-        cross(2, 0)
-        h_move(0, 3)
-        h_evac(1, 3)
-        cross(2, 1)
-        mix0(5, 0)
-        resid_v(2, 0)
-        h_evac(0, 3)
+        tanh(0, 3, 1)
+        out_turn(0, 1)
+        h_scale(3, 0)
+        load_x(x0s, x0, 5)
         out_turn(1, 1)
+        y_mm(4, 0)
+        store_out(0)
         out_evac(1, 2)
-        cross(4, 0)
-        h_quant(1, 3)
-        resid_g(2, 1)
-        mix0(5, 1)
-        resid_v(4, 0)
-        out_turn(3, 0)
-        out_turn(3, 1)
+        resid(nc.vector, 2, 0)
+        y_mm(4, 1)
+        cross(3, 0, 2); mix(4)
+        out_evac(0, 2)
+        load_x(x0s, x0, 6)
         load_x(x0s, x0, 7)
-        h_quant(0, 3)
-        out_evac(3, 2)
-        store_out(3)
-        mix1(5, 0)
-        cross(4, 1)
-        resid_v(5, 1)
+        y_mm(5, 1)
+        out_quant(0)
+        tanh(1, 3, 0)
+        stage1(1, 3, 1)
+        y_mm(5, 0)
+        out_cast(2, 0, 2)
+        resid(nc.gpsimd, 3, 1)
+        tanh(1, 3, 1)
+        resid(nc.vector, 3, 0)
         out_quant(1)
-        resid_g(2, 0)
-        out_cast(2, 0)
-        mix1(5, 1)
-        out_quant(3)
-        out_turn(2, 0)
-        y_mm(6, 0)
-        cross(5, 0)
-        mix0(6, 0)
-        resid_v(0, 1)
-        cross(5, 1)
-        resid_g(4, 0)
-        out_cast(2, 1)
-        out_cast(4, 0)
-        out_turn(4, 0)
+        h_move(3, 0)
         store_out(2)
-        resid_g(4, 1)
-        resid_v(5, 0)
-        y_mm(6, 1)
-        resid_g(5, 0)
-        out_cast(4, 1)
-        resid_g(5, 1)
-        out_cast(5, 0)
-        out_turn(4, 1)
-        mix0(6, 1)
-        store_out(4)
-        mix1(6, 0)
+        h_scale(3, 1)
+        h_evac(3, 0)
+        h_move(3, 1)
+        cross(4, 0, 2); mix(5)
+        resid(nc.gpsimd, 4, 1)
+        store_out(3)
+        h_evac(3, 1)
+        resid(nc.vector, 4, 0)
+        h_quant(3, 0, 2)
+        out_turn(2, 0)
         out_turn(2, 1)
+        y_mm(6, 0)
         out_evac(2, 2)
-        mix1(6, 1)
-        out_evac(4, 2)
-        y_mm(7, 1)
-        cross(6, 0)
-        store_out(5)
-        cross(6, 1)
-        out_quant(4)
-        resid_v(6, 0)
-        resid_v(6, 1)
-        resid_g(6, 0)
-        y_mm(7, 0)
-        mix0(7, 0)
-        mix0(7, 1)
+        out_cast(3, 0, 2)
+        y_mm(6, 1)
         out_quant(2)
-        resid_g(6, 1)
-        mix1(7, 0)
-        mix1(7, 1)
-        cross(7, 0)
-        out_cast(5, 1)
-        out_cast(6, 0)
+        out_cast(4, 0, 2)
+        out_turn(3, 0)
+        cross(5, 0, 2); mix(6)
+        out_turn(3, 1)
+        resid(nc.gpsimd, 5, 1)
+        y_mm(7, 1)
+        out_evac(3, 2)
+        y_mm(7, 0)
+        resid(nc.vector, 5, 0)
+        out_cast(5, 0, 2)
         out_turn(5, 0)
+        cross(6, 0, 2); mix(7)
+        out_turn(4, 0)
         out_turn(5, 1)
+        resid(nc.gpsimd, 6, 1)
         out_evac(5, 2)
+        out_turn(4, 1)
+        out_evac(4, 2)
+        store_out(4)
+        resid(nc.vector, 6, 0)
+        store_out(5)
+        cross(7, 0, 1)
+        out_cast(6, 0, 2)
         store_out(6)
+        out_quant(4)
         out_turn(6, 0)
-        out_cast(6, 1)
-        cross(7, 1)
+        resid(nc.vector, 7, 0)
+        out_cast(7, 0, 1)
+        out_quant(3)
         out_turn(6, 1)
-        resid_v(7, 0)
-        store_scales(0)
-        resid_v(7, 1)
+        cross(7, 1, 1)
         out_evac(6, 2)
-        out_cast(7, 0)
-        out_cast(7, 1)
         store_out(7, (0,))
         out_turn(7, 0)
-        out_quant(6)
         out_quant(5)
-        store_out(7, (1,))
+        store_scales(0)
+        resid(nc.vector, 7, 1)
         out_evac(7, 0)
+        store_out(7, (1,))
+        out_cast(7, 1, 1)
         out_turn(7, 1)
-        out_quant(7)
         out_evac(7, 1)
+        out_quant(6)
+        out_quant(7)
         out_quant(7, 1)
         store_scales(1)

from contextlib import ExitStack

import concourse.mybir as mybir
from concourse.masks import make_identity

B, D, R, E = 1024, 1024, 512, 2
FLOPS = 2 * 2 * E * B * D * R

F32 = mybir.dt.float32
BF16 = mybir.dt.bfloat16
U32 = mybir.dt.uint32
I32 = mybir.dt.int32
U8 = mybir.dt.uint8
FP8X4 = mybir.dt.float8_e4m3fn_x4
ALU = mybir.AluOpType
ACT = mybir.ActivationFunctionType
P = 128

YB, AUXB, TRB = 4, 2, 2


def tile_dcnv2lowrankexpertcross_x1_kernel(tc, x0, x, v, c, u, bias, gate, out, words, scales):
    nc = tc.nc
    with ExitStack() as ctx:
        keep = ctx.enter_context(tc.tile_pool(name="keep", bufs=1))
        work = ctx.enter_context(tc.tile_pool(name="work", bufs=2))
        psum = ctx.enter_context(tc.psum_pool(name="psum", bufs=1))
        ctx.enter_context(tc.manual_schedule())

        xs = keep.tile([P, 8, D], BF16, name="xs", align_bytes=64)
        x0s = keep.tile([P, 8, D], BF16, name="x0s", align_bytes=64)
        vraw, vg, vc, vs = {}, {}, {}, {}
        uraw, ug, uc, us = {}, {}, {}, {}
        for e in range(E):
            for g in range(2):
                vraw[e, g] = keep.tile([P, 4, R], BF16, name=f"vraw{e}{g}", align_bytes=64)
                vc[e, g] = keep.tile([P, R], U32, name=f"vc{e}{g}", align_bytes=64)
                vs[e, g] = keep.tile([P, R], U8, name=f"vs{e}{g}", align_bytes=64)
                uraw[e, g] = keep.tile([P, 4, 512], BF16, name=f"uraw{e}{g}", align_bytes=64)
                uc[e, g] = keep.tile([P, 512], U32, name=f"uc{e}{g}", align_bytes=64)
                us[e, g] = keep.tile([P, 512], U8, name=f"us{e}{g}", align_bytes=64)
        for e in range(E):
            for g in range(2):
                vg[e, g] = keep.tile([P, 4 * R], BF16, name=f"vg{e}{g}", tag="grouped", bufs=6, align_bytes=64)
        for dh in range(2):
            for e in range(E):
                ug[e, dh] = keep.tile([P, 512, 4], BF16, name=f"ug{e}{dh}", tag="grouped", bufs=6, align_bytes=64)
        xg = [keep.tile([P, 2, 256, 2], F32, name=f"xg{h}", align_bytes=64) for h in range(4)]
        xc = [keep.tile([P, 2, 256], U32, name=f"xc{h}", align_bytes=64) for h in range(4)]
        xsc = [keep.tile([P, 2, 256], U8, name=f"xsc{h}", align_bytes=64) for h in range(4)]
        hc = [keep.tile([P, E, 256], U32, name=f"hc{h}", align_bytes=64) for h in range(4)]
        hs = [keep.tile([P, E, 256], U8, name=f"hs{h}", align_bytes=64) for h in range(4)]
        osc = [keep.tile([P, 2, 512], U8, name=f"osc{h}", align_bytes=64) for h in range(2)]
        cf = keep.tile([P, E, 4], F32, name="cf")
        csb = keep.tile([P, E, 4], BF16, name="csb")
        pad = keep.tile([P, 768], BF16, name="pad")
        graw = keep.tile([P, 8, E], BF16, name="graw")
        gmx = keep.tile([P, 8], F32, name="gmx")
        gd = keep.tile([P, 8, E], F32, name="gd")
        ge = keep.tile([P, 8, E], F32, name="ge")
        gsum = keep.tile([P, 8], F32, name="gsum")
        grec = keep.tile([P, 8], F32, name="grec")
        gp = keep.tile([P, 8, E], F32, name="gp")
        bpad = keep.tile([P, D], BF16, name="bpad")
        ones = keep.tile([P, P], BF16, name="ones")
        biasb = keep.tile([P, D], F32, name="biasb")
        idf = keep.tile([P, P], F32, name="idf")
        idb = keep.tile([P, P], BF16, name="idb")
        warm = keep.tile([P, 8], F32, name="warm")

        TB = {"y": YB, "aux": AUXB, "tr": TRB}

        def bank(tag, bufs, dtype=F32, name=None):
            return psum.tile([P, 512 if dtype == F32 else 1024], dtype, name=name or tag, tag=tag, bufs=bufs)

        def load_x(dst, src, i):
            nc.sync.dma_start(out=dst[:, i, :], in_=src[i * P : (i + 1) * P, :])

        def load_v(e, g):
            nc.sync.dma_start(out=vraw[e, g][:], in_=v[e, g * 512 : (g + 1) * 512, :].rearrange("(p j) w -> p j w", j=4))

        def load_u(e, dh):
            nc.sync.dma_start(
                out=uraw[e, dh][:],
                in_=u[e, :, dh * 512 : (dh + 1) * 512].rearrange("(p j) w -> p j w", j=4),
            )

        nc.vector.memset(pad[:], 0.0)
        nc.vector.memset(bpad[:], 0.0)
        nc.vector.memset(warm[:], 0.0)
        nc.vector.memset(ones[:], 1.0)
        make_identity(nc, idb[:])
        make_identity(nc, idf[:])

        def load_bias():
            nc.scalar.dma_start(out=bpad[0:1, :], in_=bias.unsqueeze(0))

        def warm_up():
            nc.scalar.activation(out=warm[:], in_=warm[:], func=ACT.Tanh)

        def load_c():
            nc.scalar.dma_start(out=pad[0:E, 0:512], in_=c)

        def load_gate():
            nc.scalar.dma_start(out=pad[0:8, 512:768], in_=gate.rearrange("(i p) e -> i (p e)", p=P))

        small = {}

        def small_turn():
            small[0] = bank("aux", TB["aux"], BF16, name="sm")
            for t in range(4):
                nc.tensor.transpose(small[0][:, t * P : (t + 1) * P], pad[:, t:512:4], idb[:])
            for e in range(E):
                nc.tensor.transpose(small[0][:, (4 + e) * P : (5 + e) * P], pad[:, 512 + e : 768 : 2], idb[:])

        def small_evac():
            sm = small[0][:].rearrange("p (s r) -> p s r", r=P)
            nc.scalar.copy(out=csb[:].rearrange("p e t -> p t e"), in_=sm[:, 0:4, 0:E])
            nc.scalar.copy(out=graw[:].rearrange("p i e -> p e i"), in_=sm[:, 4:6, 0:8])

        xtr = {}

        def x_turn(i):
            tr = bank("tr", TB["tr"])
            trv = tr[:].rearrange("p (g u r) -> p g u r", g=2, u=2)
            xw = xs[:, i, :].bitcast(F32)
            for g in range(2):
                for w in range(2):
                    nc.tensor.transpose(trv[:, g, w, :], xw[:, 256 * g + w : 256 * (g + 1) : 2], idf[:])
            xtr[i] = tr

        def x_evac(i):
            li = i % 2
            nc.scalar.copy(
                out=xg[i // 2][:, :, li * P : (li + 1) * P, :], in_=xtr[i][:].rearrange("p (g u r) -> p g r u", g=2, u=2)
            )

        def x_quant(h):
            nc.vector.quantize_mx(
                out=xc[h][:].rearrange("p g b -> p (g b)").bitcast(FP8X4),
                scales=xsc[h][:].rearrange("p g b -> p (g b)"),
                in_=xg[h][:].rearrange("p g b u -> p (g b u)").bitcast(BF16),
            )

        mvs = {}

        def move(tag, key, rows):
            mv = bank(tag, TB[tag], BF16, name="mv")
            mvs[key] = mv[:].rearrange("p (j c) -> p j c", j=4)
            for k in range(2):
                nc.tensor.matmul(
                    mvs[key][:, 2 * k : 2 * k + 2, :], lhsT=idb[:], rhs=rows[:, 2 * k : 2 * k + 2, :], start=True, stop=True
                )

        def vdst(e, g, q):
            return vg[e, g][:].rearrange("p (t m j) -> p t m j", t=4, j=4)[:, :, 64 * q : 64 * (q + 1), :]

        def v_inter(e, g):
            nc.vector.tensor_copy(
                out=vg[e, g][:].rearrange("p (t m j) -> p t m j", t=4, j=4),
                in_=vraw[e, g][:].rearrange("p j (m t) -> p t m j", t=4),
            )

        def v_move(e, g, q, tag="y"):
            move(tag, ("v", e, g, q), vraw[e, g][:, :, 256 * q : 256 * (q + 1)])

        def v_evac(e, g, q):
            nc.scalar.copy(out=vdst(e, g, q), in_=mvs["v", e, g, q].rearrange("p j (m t) -> p t m j", t=4))

        def v_quant(e, g):
            nc.vector.quantize_mx(out=vc[e, g][:].bitcast(FP8X4), scales=vs[e, g][:], in_=vg[e, g][:])

        def u_move(e, dh, q, tag="y"):
            move(tag, ("u", e, dh, q), uraw[e, dh][:, :, 256 * q : 256 * (q + 1)])

        def u_evac(e, dh, q):
            nc.scalar.copy(out=ug[e, dh][:, 256 * q : 256 * (q + 1), :], in_=mvs["u", e, dh, q].rearrange("p j c -> p c j"))

        def u_inter(e, dh, q):
            cols = slice(256 * q, 256 * (q + 1))
            nc.scalar.copy(out=ug[e, dh][:, cols, :], in_=uraw[e, dh][:, :, cols].rearrange("p j c -> p c j"))

        def u_quant(e, dh):
            nc.vector.quantize_mx(
                out=uc[e, dh][:].bitcast(FP8X4), scales=us[e, dh][:], in_=ug[e, dh][:].rearrange("p c j -> p (c j)")
            )

        th, acc1, hb, ht = {}, {}, {}, {}

        def stage1(e, h, q):
            acc1[e, h, q] = bank("aux", TB["aux"], name="a1")
            for k in range(2):
                t = 2 * q + k
                for g in range(2):
                    nc.tensor.matmul_mx(
                        out=acc1[e, h, q][:, 256 * k : 256 * (k + 1)],
                        lhsT=vc[e, g][:, t * P : (t + 1) * P].bitcast(FP8X4),
                        lhsT_scale=vs[e, g][:, t * P : (t + 1) * P],
                        rhs=xc[h][:, g, :].bitcast(FP8X4),
                        rhs_scale=xsc[h][:, g, :],
                        start=(g == 0),
                        stop=(g == 1),
                    )

        def tanh(e, h, q):
            if e == 0 and q == 0:
                th[h] = work.tile([P, E, 4, 256], F32, name="th", tag="th", bufs=2)
            nc.scalar.activation(
                out=th[h][:, e, 2 * q : 2 * q + 2, :].rearrange("p t b -> p (t b)"), in_=acc1[e, h, q][:], func=ACT.Tanh
            )

        def new_hb(h):
            hb[h] = work.tile([P, E, 256, 4], BF16, name="hb", tag="hb", bufs=2, align_bytes=64)

        def h_mult(h, e0, n):
            if e0 == 0:
                new_hb(h)
            nc.vector.tensor_tensor(
                out=hb[h][:, e0 : e0 + n, :, :],
                in0=th[h][:, e0 : e0 + n, :, :].rearrange("p e t b -> p e b t"),
                in1=csb[:, e0 : e0 + n, :].unsqueeze(2).to_broadcast([P, n, 256, 4]),
                op=ALU.mult,
            )

        def h_scale(h, e):
            if e == 0:
                ht[h] = work.tile([P, E, 4, 256], BF16, name="ht", tag="ht", bufs=1)
            for t in range(4):
                nc.scalar.activation(out=ht[h][:, e, t, :], in_=th[h][:, e, t, :], func=ACT.Copy, scale=cf[:, e, t : t + 1])

        def h_inter(h, e):
            if e == 0:
                new_hb(h)
            nc.scalar.copy(out=hb[h][:, e, :, :], in_=ht[h][:, e, :, :].rearrange("p t b -> p b t"))

        def h_move(h, e):
            move("aux", ("h", e, h), ht[h][:, e, :, :])

        def h_evac(h, e):
            if e == 0:
                new_hb(h)
            nc.scalar.copy(out=hb[h][:, e, :, :], in_=mvs["h", e, h].rearrange("p t b -> p b t"))

        def h_quant(h, e0, n):
            nc.vector.quantize_mx(
                out=hc[h][:, e0 : e0 + n, :].rearrange("p e b -> p (e b)").bitcast(FP8X4),
                scales=hs[h][:, e0 : e0 + n, :].rearrange("p e b -> p (e b)"),
                in_=hb[h][:, e0 : e0 + n, :, :].rearrange("p e b t -> p (e b t)"),
            )

        pairs = [(0, 0), (2, 0), (0, 1), (2, 1), (4, 0), (4, 1), (6, 0), (6, 1)]
        N = len(pairs)
        ys, sa, ot, qb = {}, {}, {}, {}

        def y_mm(k, e):
            i0, dh = pairs[k]
            if True:
                for a in range(2):
                    i = i0 + a
                    h, li = i // 2, i % 2
                    ys[k, e, a] = bank("y", TB["y"], name="y")
                    nc.tensor.matmul_mx(
                        out=ys[k, e, a][:],
                        lhsT=hc[h][:, e, li * P : (li + 1) * P].bitcast(FP8X4),
                        lhsT_scale=hs[h][:, e, li * P : (li + 1) * P],
                        rhs=uc[e, dh][:].bitcast(FP8X4),
                        rhs_scale=us[e, dh][:],
                        start=True,
                        stop=True,
                    )

        def mix0(k, a):
            i0, dh = pairs[k]
            if a == 0:
                sa[k] = [work.tile([P, 2, 512], F32, name=f"s{n}", tag=f"s{n}") for n in range(3)]
            nc.vector.scalar_tensor_tensor(
                out=sa[k][0][:, a, :], in0=ys[k, 0, a][:], scalar=gp[:, i0 + a, 0:1],
                in1=biasb[:, dh * 512 : (dh + 1) * 512], op0=ALU.mult, op1=ALU.add,
            )

        def mix1(k, a):
            i0, dh = pairs[k]
            nc.vector.scalar_tensor_tensor(
                out=sa[k][1][:, a, :], in0=ys[k, 1, a][:], scalar=gp[:, i0 + a, 1:2],
                in1=sa[k][0][:, a, :], op0=ALU.mult, op1=ALU.add,
            )

        def mix(k):
            for a in range(2):
                mix0(k, a)
            for a in range(2):
                mix1(k, a)

        def cross(k, a0, n):
            i0, dh = pairs[k]
            cols = slice(dh * 512, (dh + 1) * 512)
            nc.vector.tensor_tensor(
                out=sa[k][2][:, a0 : a0 + n, :], in0=sa[k][1][:, a0 : a0 + n, :], in1=x0s[:, i0 + a0 : i0 + a0 + n, cols], op=ALU.mult
            )
            if a0 == 0:
                ot[k] = work.tile([P, 2, 512], F32, name="ot", tag="ot", bufs=3)

        def resid(eng, k, a):
            i0, dh = pairs[k]
            eng.tensor_tensor(
                out=ot[k][:, a, :], in0=sa[k][2][:, a, :], in1=xs[:, i0 + a, dh * 512 : (dh + 1) * 512], op=ALU.add
            )

        def store_out(k, which=(0, 1)):
            i0, dh = pairs[k]
            lo, n = which[0], len(which)
            nc.sync.dma_start(
                out=out[(i0 + lo) * P : (i0 + lo + n) * P, dh * 512 : (dh + 1) * 512].rearrange("(i p) d -> p i d", p=P),
                in_=ot[k][:, lo : lo + n, :],
            )

        otr = {}

        cb = {}

        def out_cast(k, a0, n):
            if a0 == 0:
                cb[k] = work.tile([P, 2, 256], F32, name="cb", tag="cb", bufs=2)
            nc.scalar.copy(
                out=cb[k][:, :, P * a0 : P * (a0 + n)].bitcast(BF16).rearrange("p u (m w) -> p u m w", w=2),
                in_=ot[k][:, a0 : a0 + n, :].rearrange("p a (m u w) -> p u (a m) w", u=2, w=2),
            )

        def out_turn(k, a):
            if a == 0:
                otr[k] = bank("tr", TB["tr"])
            for w in range(2):
                nc.tensor.transpose(
                    otr[k][:, (2 * a + w) * P : (2 * a + w + 1) * P], cb[k][:, w, a * P : (a + 1) * P], idf[:]
                )

        def out_evac(k, a):
            if a != 1:
                qb[k] = work.tile([P, 256, 2], F32, name="qb", tag="qb", bufs=3, align_bytes=64)
            if a == 2:
                nc.scalar.copy(
                    out=qb[k][:].rearrange("p (a r) u -> p a r u", a=2),
                    in_=otr[k][:].rearrange("p (a u r) -> p a r u", a=2, u=2),
                )
            else:
                nc.scalar.copy(
                    out=qb[k][:, a * P : (a + 1) * P, :],
                    in_=otr[k][:, 256 * a : 256 * (a + 1)].rearrange("p (u r) -> p r u", u=2),
                )

        wqs = {}

        def out_quant(k, a=0):
            i0, dh = pairs[k]
            if a == 0:
                wqs[k] = work.tile([P, 256], U32, name="wq", tag="wq", bufs=3, align_bytes=64)
            wq = wqs[k]
            parts = 2 if k == N - 1 else 1
            n = 256 // parts
            if True:
                r0 = i0 * P + n * a
                nc.vector.quantize_mx(
                    out=wq[:, n * a : n * (a + 1)].bitcast(FP8X4), scales=osc[r0 // 512][:, dh, r0 % 512 : r0 % 512 + n],
                    in_=qb[k][:, n * a : n * (a + 1), :].rearrange("p b u -> p (b u)").bitcast(BF16),
                )
                nc.sync.dma_start(
                    out=words[dh, :, r0 : r0 + n, :].rearrange("p m t -> p (m t)").bitcast(I32),
                    in_=wq[:, n * a : n * (a + 1)].bitcast(I32),
                )

        def store_scales(h):
            cols = slice(512 * h, 512 * (h + 1))
            for q in range(4):
                nc.sync.dma_start(
                    out=scales[:, 4 * q : 4 * q + 4, cols].rearrange("g q m -> q g m").bitcast(I32),
                    in_=osc[h][32 * q : 32 * q + 4, :, :].bitcast(I32),
                )

        bbs = {}

        def bias_mm(dh):
            bbs[dh] = bank("aux", TB["aux"], name="bb")
            nc.tensor.matmul(bbs[dh][:], lhsT=ones[:], rhs=bpad[:, dh * 512 : (dh + 1) * 512], start=True, stop=True)

        def bias_evac(dh):
            nc.scalar.copy(out=biasb[:, dh * 512 : (dh + 1) * 512], in_=bbs[dh][:])

        def gate1():
            nc.vector.tensor_tensor(out=gmx[:], in0=graw[:, :, 0], in1=graw[:, :, 1], op=ALU.max)

        def gate2():
            nc.gpsimd.tensor_tensor(
                out=gd[:], in0=graw[:], in1=gmx[:].unsqueeze(2).to_broadcast([P, 8, E]), op=ALU.subtract
            )

        def gate3():
            nc.scalar.activation(out=ge[:], in_=gd[:], func=ACT.Exp)

        def gate4():
            nc.gpsimd.tensor_tensor(out=gsum[:], in0=ge[:, :, 0], in1=ge[:, :, 1], op=ALU.add)

        def gate5():
            nc.vector.reciprocal(out=grec[:], in_=gsum[:])

        def gate6():
            nc.gpsimd.tensor_tensor(out=gp[:], in0=ge[:], in1=grec[:].unsqueeze(2).to_broadcast([P, 8, E]), op=ALU.mult)

        def cf_copy():
            nc.gpsimd.tensor_copy(out=cf[:], in_=csb[:])

        def h_mult_g(e, h):
            new_hb(e, h)
            nc.gpsimd.tensor_tensor(
                out=hb[e, h][:],
                in0=th[e, h][:].rearrange("p t b -> p b t"),
                in1=csb[:, e, :].unsqueeze(1).to_broadcast([P, 256, 4]),
                op=ALU.mult,
            )

        load_v(0, 0)
        load_x(xs, x, 0)
        load_x(xs, x, 1)
        load_v(0, 1)
        load_c()
        load_gate()
        load_bias()
        warm_up()
        load_v(1, 0)
        x_turn(0)
        v_inter(0, 0)
        v_quant(0, 0)
        load_v(1, 1)
        x_turn(1)
        small_turn()
        x_evac(0)
        load_u(0, 0)
        v_inter(0, 1)
        small_evac()
        load_u(1, 0)
        bias_mm(0)
        gate1()
        bias_mm(1)
        x_evac(1)
        v_quant(0, 1)
        x_quant(0)
        bias_evac(0)
        gate2()
        v_move(1, 1, 0)
        bias_evac(1)
        v_move(1, 1, 1)
        gate3()
        v_evac(1, 1, 0)
        stage1(0, 0, 0)
        v_evac(1, 1, 1)
        u_move(0, 0, 0)
        stage1(0, 0, 1)
        u_move(0, 0, 1)
        gate4()
        load_x(xs, x, 2)
        v_inter(1, 0)
        gate5()
        load_x(xs, x, 3)
        v_quant(1, 0)
        v_quant(1, 1)
        load_x(x0s, x0, 0)
        x_turn(2)
        tanh(0, 0, 0)
        u_evac(0, 0, 0)
        gate6()
        load_x(x0s, x0, 1)
        load_u(0, 1)
        load_u(1, 1)
        x_turn(3)
        tanh(0, 0, 1)
        u_evac(0, 0, 1)
        h_mult(0, 0, 1)
        stage1(1, 0, 1)
        stage1(1, 0, 0)
        x_evac(2)
        u_move(1, 0, 0)
        load_x(x0s, x0, 2)
        load_x(x0s, x0, 3)
        x_evac(3)
        tanh(1, 0, 1)
        u_move(1, 0, 1)
        tanh(1, 0, 0)
        u_quant(0, 0)
        x_quant(1)
        u_evac(1, 0, 0)
        h_quant(0, 0, 1)
        stage1(0, 1, 0)
        h_mult(0, 1, 1)
        stage1(1, 1, 1)
        load_x(xs, x, 4)
        u_evac(1, 0, 1)
        tanh(0, 1, 0)
        u_quant(1, 0)
        h_quant(0, 1, 1)
        load_x(xs, x, 5)
        y_mm(0, 0)
        load_x(xs, x, 6)
        tanh(1, 1, 1)
        load_x(xs, x, 7)
        stage1(0, 1, 1)
        cf_copy()
        tanh(0, 1, 1)
        stage1(1, 1, 0)
        y_mm(0, 1)
        x_turn(4)
        x_turn(5)
        mix(0)
        tanh(1, 1, 0)
        u_inter(0, 1, 0)
        h_mult(1, 0, 2)
        x_evac(4)
        x_turn(7)
        x_evac(5)
        u_inter(0, 1, 1)
        x_quant(2)
        h_quant(1, 0, 2)
        x_turn(6)
        stage1(0, 2, 0)
        u_quant(0, 1)
        y_mm(1, 0)
        y_mm(1, 1)
        u_inter(1, 1, 0)
        x_evac(6)
        tanh(0, 2, 0)
        u_inter(1, 1, 1)
        cross(0, 0, 2); mix(1)
        u_quant(1, 1)
        x_evac(7)
        stage1(0, 2, 1)
        tanh(0, 2, 1)
        resid(nc.gpsimd, 0, 1)
        stage1(1, 2, 1)
        resid(nc.vector, 0, 0)
        y_mm(2, 0)
        load_x(x0s, x0, 4)
        tanh(1, 2, 1)
        stage1(1, 2, 0)
        x_quant(3)
        y_mm(2, 1)
        h_scale(2, 0)
        cross(1, 0, 2); mix(2)
        resid(nc.gpsimd, 1, 1)
        stage1(0, 3, 0)
        tanh(1, 2, 0)
        h_scale(2, 1)
        resid(nc.vector, 1, 0)
        h_move(2, 0)
        y_mm(3, 0)
        store_out(1)
        y_mm(3, 1)
        cross(2, 0, 2); mix(3)
        tanh(0, 3, 0)
        out_cast(0, 0, 2)
        h_move(2, 1)
        out_turn(0, 0)
        h_evac(2, 0)
        h_evac(2, 1)
        h_quant(2, 0, 2)
        stage1(0, 3, 1)
        stage1(1, 3, 0)
        out_cast(1, 0, 2)
        resid(nc.gpsimd, 2, 1)
        out_turn(1, 0)
        tanh(0, 3, 1)
        out_turn(0, 1)
        h_scale(3, 0)
        load_x(x0s, x0, 5)
        out_turn(1, 1)
        y_mm(4, 0)
        store_out(0)
        out_evac(1, 2)
        resid(nc.vector, 2, 0)
        y_mm(4, 1)
        cross(3, 0, 2); mix(4)
        out_evac(0, 2)
        load_x(x0s, x0, 6)
        load_x(x0s, x0, 7)
        y_mm(5, 1)
        out_quant(0)
        tanh(1, 3, 0)
        stage1(1, 3, 1)
        y_mm(5, 0)
        out_cast(2, 0, 2)
        resid(nc.gpsimd, 3, 1)
        tanh(1, 3, 1)
        resid(nc.vector, 3, 0)
        out_quant(1)
        h_move(3, 0)
        store_out(2)
        h_scale(3, 1)
        h_evac(3, 0)
        h_move(3, 1)
        cross(4, 0, 2); mix(5)
        resid(nc.gpsimd, 4, 1)
        store_out(3)
        h_evac(3, 1)
        resid(nc.vector, 4, 0)
        h_quant(3, 0, 2)
        out_turn(2, 0)
        out_turn(2, 1)
        y_mm(6, 0)
        out_evac(2, 2)
        out_cast(3, 0, 2)
        y_mm(6, 1)
        out_quant(2)
        out_cast(4, 0, 2)
        out_turn(3, 0)
        cross(5, 0, 2); mix(6)
        out_turn(3, 1)
        resid(nc.gpsimd, 5, 1)
        y_mm(7, 1)
        out_evac(3, 2)
        y_mm(7, 0)
        resid(nc.vector, 5, 0)
        out_cast(5, 0, 2)
        out_turn(5, 0)
        cross(6, 0, 2); mix(7)
        out_turn(4, 0)
        out_turn(5, 1)
        resid(nc.gpsimd, 6, 1)
        out_evac(5, 2)
        out_turn(4, 1)
        out_evac(4, 2)
        store_out(4)
        resid(nc.vector, 6, 0)
        store_out(5)
        cross(7, 0, 1)
        out_cast(6, 0, 2)
        store_out(6)
        out_quant(4)
        out_turn(6, 0)
        resid(nc.vector, 7, 0)
        out_cast(7, 0, 1)
        out_quant(3)
        out_turn(6, 1)
        cross(7, 1, 1)
        out_evac(6, 2)
        store_out(7, (0,))
        out_turn(7, 0)
        out_quant(5)
        store_scales(0)
        resid(nc.vector, 7, 1)
        out_evac(7, 0)
        store_out(7, (1,))
        out_cast(7, 1, 1)
        out_turn(7, 1)
        out_evac(7, 1)
        out_quant(6)
        out_quant(7)
        out_quant(7, 1)
        store_scales(1)
